import numpy as np
import ml_dtypes


def mxq(x, axis, fmt="e4m3"):
    dtype, down = {"e4m3": (ml_dtypes.float8_e4m3fn, 7), "e5m2": (ml_dtypes.float8_e5m2, 14)}[fmt]
    v = np.moveaxis(np.asarray(x, np.float32).astype(ml_dtypes.bfloat16).astype(np.float64), axis, -1)
    blocks = v.reshape(v.shape[:-1] + (-1, 32))
    amax = np.abs(blocks).max(-1, keepdims=True)
    byte = np.maximum(np.where(amax > 0, np.frexp(amax)[1] - 1 + 127, 0) - down, 1)
    scale = np.exp2(byte - 127.0)
    codes = (blocks / scale).astype(np.float32).astype(dtype).astype(np.float64)
    return np.moveaxis((codes * scale).reshape(v.shape), -1, axis)


WIDE = False


def mx_kscale(k):
    if not WIDE:
        return np.ones(k)
    levels = np.array([10, -10, 5, -5, 0])
    if k % 512:
        return np.exp2(np.random.permutation(np.resize(levels, k // 32))).repeat(32)
    a = np.empty((k // 512, 16))
    for p in range(k // 512):
        a[p, :8] = np.random.permutation(np.resize(levels, 8))
        for g in range(8):
            far = levels[np.abs(levels - a[p, g]) >= 10]
            a[p, g + 8] = far[np.random.randint(len(far))]
    return np.exp2(a.ravel()).repeat(32)


def f64(x):
    return np.asarray(x).astype(np.float64)


def striped(idx):
    return np.tile(np.asarray(idx).reshape(-1, 16).T, (8, 1)).astype(np.uint16)


def unstriped(offs):
    return offs[:16].T.reshape(-1).astype(np.int64)


E2M1 = np.array([0.0, 0.5, 1.0, 1.5, 2.0, 3.0, 4.0, 6.0, -0.0, -0.5, -1.0, -1.5, -2.0, -3.0, -4.0, -6.0])


def pack_weight(w, fmt):
    k, n = w.shape
    w = f64(np.asarray(w, np.float32).astype(ml_dtypes.bfloat16)).reshape(k // 32, 32, n)
    amax = np.abs(w).max(1)
    if fmt == "e4m3":
        byte = np.frexp(amax)[1] - 1 + 127 - 7
    else:
        mant, ex = np.frexp(amax / 6.0)
        byte = np.where(mant > 0.5, ex, ex - 1) + 127
    byte = np.clip(np.where(amax > 0, byte, 1), 1, 254)
    scaled = (w * np.exp2(127.0 - byte)[:, None, :]).reshape(k, n).astype(np.float32)
    by_word = np.ascontiguousarray(scaled.reshape(k // 512, 128, 4, n).transpose(0, 1, 3, 2))
    if fmt == "e4m3":
        words = by_word.astype(ml_dtypes.float8_e4m3fn).view(np.uint8)
    else:
        c = by_word.astype(ml_dtypes.float4_e2m1fn).view(np.uint8) & 0xF
        words = (c[..., 0::2] | (c[..., 1::2] << 4)).reshape(k // 512, 128, 2 * n)
    return np.ascontiguousarray(words), np.ascontiguousarray(byte.astype(np.uint8).reshape(k // 512, 16, n))


def unpack_weight(words, scales, fmt):
    g, _, n = scales.shape
    words = np.ascontiguousarray(words).reshape(g, 128, n, -1)
    if fmt == "e4m3":
        vals = words.view(ml_dtypes.float8_e4m3fn).astype(np.float64)
    else:
        nib = np.empty((g, 128, n, 4), np.uint8)
        nib[..., 0::2] = words & 0xF
        nib[..., 1::2] = words >> 4
        vals = E2M1[nib]
    vals = vals * np.repeat(np.exp2(scales.astype(np.float64) - 127.0), 8, axis=1)[..., None]
    return vals.transpose(0, 1, 3, 2).reshape(g * 512, n)


def sigmoid(v):
    return 1.0 / (1.0 + np.exp(-v))


B, N, T, D, NQ = 1, 512, 2048, 512, 256


def setup_inputs():
    n = np.random.standard_normal
    idx = np.sort(np.random.permutation(T)[:B * N].reshape(B, N), axis=1).reshape(-1)
    s = mx_kscale(D)[:, None]
    kp = pack_weight(n((D, T)) / s, "e4m3")
    return {
        "qT": (n((B, D, NQ)) * s * (1.00 / np.sqrt(D))).astype(np.float32),
        "k_words": kp[0],
        "k_scales": kp[1],
        "ts": np.tile(np.random.uniform(0.5, 2.0, 2048), (128, 1)).astype(np.float32),
        "pr": np.tile(np.random.uniform(0.1, 1.0, 2048), (128, 1)).astype(np.float32),
        "offs": striped(idx),
    }


def reference(qT, k_words, k_scales, ts, pr, offs):
    idx = unstriped(offs)
    pick = lambda x, which: x[:, which].reshape(x.shape[0], B, -1).transpose(1, 0, 2)
    k = unpack_weight(k_words, k_scales, "e4m3")
    kg = pick(k, idx)
    qq = mxq(f64(qT), 1, "e4m3")
    a = qq.transpose(0, 2, 1) @ kg
    y = sigmoid(a * pick(f64(ts), idx)[:, :1, :]) * pick(f64(pr), idx)[:, :1, :]
    return y

@@ -1,0 +1,132 @@
+from contextlib import ExitStack
+
+import concourse.mybir as mybir
+from concourse.masks import make_identity
+
+NQ, N, T, D = 256, 512, 2048, 512
+FLOPS = 2 * NQ * N * D
+BYTES = 4 * D * NQ + D * T + 16 * T + 2 * 4 * T + 128 * (N // 16) * 2 + 4 * NQ * N
+
+F32 = mybir.dt.float32
+BF16 = mybir.dt.bfloat16
+I32 = mybir.dt.int32
+U32 = mybir.dt.uint32
+U16 = mybir.dt.uint16
+U8 = mybir.dt.uint8
+FP8X4 = mybir.dt.float8_e4m3fn_x4
+MULT = mybir.AluOpType.mult
+SIGMOID = mybir.ActivationFunctionType.Sigmoid
+
+P = 128
+PACK = 4
+LAST = P - 1
+HALF = N // 2
+BLOCKS = N // P
+PR_SPLIT = 512
+
+
+def tile_attend_sigprior_srt_kernel(tc, qT, k_words, k_scales, ts, pr, offs, out):
+    nc = tc.nc
+    with ExitStack() as ctx:
+        sb = ctx.enter_context(tc.tile_pool(name="sb", bufs=1))
+        ps = ctx.enter_context(tc.psum_pool(name="ps", bufs=1))
+
+        offsets = sb.tile([P, N // 16], U16, name="offsets")
+        ks_pool = sb.tile([P, T // 4], I32, name="ks_pool", align_bytes=64)
+        ts_pool = sb.tile([P, T], F32, name="ts_pool", align_bytes=64)
+        pr_pool = sb.tile([P, T], F32, name="pr_pool", align_bytes=64)
+        kw_pool = sb.tile([P, T], I32, name="kw_pool", align_bytes=64)
+        q_raw = sb.tile([P, PACK, NQ], F32, name="q_raw", align_bytes=64)
+        ident = sb.tile([P, P], F32, name="ident", align_bytes=64)
+        warm = sb.tile([P, 1], F32, name="warm")
+        warm_out = sb.tile([P, 1], F32, name="warm_out")
+
+        nc.sync.dma_start(offsets[:], offs)
+        nc.sync.dma_start(ts_pool[LAST:P, :], ts[0:1, :])
+        nc.sync.dma_start(q_raw[:], qT[0].rearrange("(p j) w -> p j w", j=PACK))
+        nc.sync.dma_start(kw_pool[:], k_words[0].rearrange("p n t -> p (n t)").bitcast(I32))
+
+        nc.vector.memset(ks_pool[:], 0)
+        nc.scalar.dma_start(pr_pool[LAST:P, :], pr[0:1, :])
+        for quad in range(4):
+            nc.scalar.dma_start(ks_pool[32 * quad : 32 * quad + 4, :], k_scales[0, 4 * quad : 4 * quad + 4, :].bitcast(I32))
+        nc.gpsimd.memset(warm[:], 0.0)
+        nc.scalar.activation(warm_out[:], warm[:], SIGMOID)
+        make_identity(nc, ident[:])
+        nc.vector.memset(ts_pool[0:LAST, :], 0.0)
+        nc.vector.memset(pr_pool[0:LAST, 0:PR_SPLIT], 0.0)
+        nc.gpsimd.memset(pr_pool[0:LAST, PR_SPLIT - 8 : T], 0.0)
+
+        def halves(h):
+            return slice(h * HALF, (h + 1) * HALF), offsets[:, h * (HALF // 16) : (h + 1) * (HALF // 16)]
+
+        def turn(rows, turned, h):
+            for b in (2 * h, 2 * h + 1):
+                nc.tensor.transpose(turned[:, b, :], rows[:, b * P : (b + 1) * P], ident[:])
+
+        def spread(turned, name):
+            column = sb.tile([P, BLOCKS], F32, name=name + "_column")
+            nc.scalar.copy(column[:], turned[:, :, LAST])
+            wide = ps.tile([P, N], F32, name=name + "_wide")
+            for b in range(BLOCKS):
+                nc.tensor.transpose(wide[:, b * P : (b + 1) * P], column[:, b : b + 1].to_broadcast([P, P]), ident[:])
+            return wide
+
+        ts_rows = sb.tile([P, N], F32, name="ts_rows", align_bytes=64)
+        ts_turned = ps.tile([P, BLOCKS, P], F32, name="ts_turned")
+        for h in range(2):
+            cols, offs_h = halves(h)
+            nc.vector.tensor_copy(ts_rows[:, cols], ts_pool[:].indirect(offs_h))
+            turn(ts_rows, ts_turned, h)
+
+        q_bf = sb.tile([P, NQ, PACK], BF16, name="q_bf", align_bytes=64)
+        nc.scalar.copy(q_bf[:, 0:P, :], q_raw[:, :, 0:P].rearrange("p j w -> p w j"))
+        ts_wide = spread(ts_turned, "ts")
+        nc.scalar.copy(q_bf[:, P:NQ, :], q_raw[:, :, P:NQ].rearrange("p j w -> p w j"))
+        ts_sb = sb.tile([P, N], F32, name="ts_sb", align_bytes=64)
+        nc.scalar.copy(ts_sb[:], ts_wide[:])
+
+        ks = sb.tile([P, N], U8, name="ks", align_bytes=64)
+        nc.vector.tensor_copy(ks[:], ks_pool[:].bitcast(U8).indirect(offsets[:]))
+
+        pr_rows = sb.tile([P, N], F32, name="pr_rows", align_bytes=64)
+        pr_turned = ps.tile([P, BLOCKS, P], F32, name="pr_turned")
+        nc.vector.tensor_copy(pr_rows[:], pr_pool[:].indirect(offsets[:]))
+        for h in range(2):
+            turn(pr_rows, pr_turned, h)
+
+        q_codes = sb.tile([P, NQ], U32, name="q_codes", align_bytes=64)
+        q_scales = sb.tile([P, NQ], U8, name="q_scales", align_bytes=64)
+        nc.vector.quantize_mx(q_codes[:].bitcast(FP8X4), q_scales[:], q_bf[:].rearrange("p w j -> p (w j)"))
+        pr_wide = spread(pr_turned, "pr")
+
+        kw = [sb.tile([P, HALF], U32, name=f"kw{h}", align_bytes=64) for h in range(2)]
+        for h in range(2):
+            nc.vector.tensor_copy(kw[h][:], kw_pool[:].bitcast(U32).indirect(halves(h)[1]))
+
+        parts = [(h, g) for h in range(2) for g in range(2)]
+        scores, scaled, weight = {}, {}, {}
+        for h, g in parts:
+            cols = halves(h)[0]
+            rows = slice(g * P, (g + 1) * P)
+            scores[h, g] = ps.tile([P, HALF], F32, name=f"scores{h}{g}")
+            nc.tensor.matmul_mx(
+                scores[h, g][:],
+                lhsT=q_codes[:, rows].bitcast(FP8X4),
+                lhsT_scale=q_scales[:, rows],
+                rhs=kw[h][:].bitcast(FP8X4),
+                rhs_scale=ks[:, cols],
+                start=True,
+                stop=True,
+            )
+        for h, g in parts:
+            cols = halves(h)[0]
+            scaled[h, g] = sb.tile([P, HALF], F32, name=f"scaled{h}{g}")
+            nc.vector.tensor_tensor(scaled[h, g][:], scores[h, g][:], ts_sb[:, cols], MULT)
+            weight[h, g] = sb.tile([P, HALF], F32, name=f"weight{h}{g}")
+            nc.scalar.activation(weight[h, g][:], scaled[h, g][:], SIGMOID)
+        for h, g in parts:
+            cols = halves(h)[0]
+            result = sb.tile([P, HALF], F32, name=f"result{h}{g}")
+            nc.vector.tensor_tensor(result[:], weight[h, g][:], pr_wide[:, cols], MULT)
+            nc.sync.dma_start(out[0, g * P : (g + 1) * P, cols], result[:])

@@ -22,7 +22,6 @@ PACK = 4
 LAST = P - 1
 HALF = N // 2
 BLOCKS = N // P
-PR_SPLIT = 512
 
 
 def tile_attend_sigprior_srt_kernel(tc, qT, k_words, k_scales, ts, pr, offs, out):
@@ -42,27 +41,32 @@ def tile_attend_sigprior_srt_kernel(tc, qT, k_words, k_scales, ts, pr, offs, out
         warm_out = sb.tile([P, 1], F32, name="warm_out")
 
         nc.sync.dma_start(offsets[:], offs)
-        nc.sync.dma_start(ts_pool[LAST:P, :], ts[0:1, :])
         nc.sync.dma_start(q_raw[:], qT[0].rearrange("(p j) w -> p j w", j=PACK))
         nc.sync.dma_start(kw_pool[:], k_words[0].rearrange("p n t -> p (n t)").bitcast(I32))
 
         nc.vector.memset(ks_pool[:], 0)
+        nc.gpsimd.memset(warm[:], 0.0)
+        nc.scalar.dma_start(ts_pool[LAST:P, :], ts[0:1, :])
         nc.scalar.dma_start(pr_pool[LAST:P, :], pr[0:1, :])
         for quad in range(4):
+            if quad == 3:
+                nc.scalar.activation(warm_out[:], warm[:], SIGMOID)
             nc.scalar.dma_start(ks_pool[32 * quad : 32 * quad + 4, :], k_scales[0, 4 * quad : 4 * quad + 4, :].bitcast(I32))
-        nc.gpsimd.memset(warm[:], 0.0)
-        nc.scalar.activation(warm_out[:], warm[:], SIGMOID)
-        make_identity(nc, ident[:])
         nc.vector.memset(ts_pool[0:LAST, :], 0.0)
-        nc.vector.memset(pr_pool[0:LAST, 0:PR_SPLIT], 0.0)
-        nc.gpsimd.memset(pr_pool[0:LAST, PR_SPLIT - 8 : T], 0.0)
+        nc.vector.memset(pr_pool[0:LAST, :], 0.0)
+        nc.vector.memset(ident[:], 0.0)
+        make_identity(nc, ident[:], nomemset=True)
 
         def halves(h):
             return slice(h * HALF, (h + 1) * HALF), offsets[:, h * (HALF // 16) : (h + 1) * (HALF // 16)]
 
-        def turn(rows, turned, h):
-            for b in (2 * h, 2 * h + 1):
+        def turn(pool, name):
+            rows = sb.tile([P, N], F32, name=name + "_rows", align_bytes=64)
+            nc.vector.tensor_copy(rows[:], pool[:].indirect(offsets[:]))
+            turned = ps.tile([P, BLOCKS, P], F32, name=name + "_turned")
+            for b in range(BLOCKS):
                 nc.tensor.transpose(turned[:, b, :], rows[:, b * P : (b + 1) * P], ident[:])
+            return turned
 
         def spread(turned, name):
             column = sb.tile([P, BLOCKS], F32, name=name + "_column")
@@ -72,33 +76,22 @@ def tile_attend_sigprior_srt_kernel(tc, qT, k_words, k_scales, ts, pr, offs, out
                 nc.tensor.transpose(wide[:, b * P : (b + 1) * P], column[:, b : b + 1].to_broadcast([P, P]), ident[:])
             return wide
 
-        ts_rows = sb.tile([P, N], F32, name="ts_rows", align_bytes=64)
-        ts_turned = ps.tile([P, BLOCKS, P], F32, name="ts_turned")
-        for h in range(2):
-            cols, offs_h = halves(h)
-            nc.vector.tensor_copy(ts_rows[:, cols], ts_pool[:].indirect(offs_h))
-            turn(ts_rows, ts_turned, h)
-
         q_bf = sb.tile([P, NQ, PACK], BF16, name="q_bf", align_bytes=64)
-        nc.scalar.copy(q_bf[:, 0:P, :], q_raw[:, :, 0:P].rearrange("p j w -> p w j"))
+        nc.scalar.copy(q_bf[:], q_raw[:].rearrange("p j w -> p w j"))
+
+        ts_turned = turn(ts_pool, "ts")
+        pr_turned = turn(pr_pool, "pr")
         ts_wide = spread(ts_turned, "ts")
-        nc.scalar.copy(q_bf[:, P:NQ, :], q_raw[:, :, P:NQ].rearrange("p j w -> p w j"))
+        pr_wide = spread(pr_turned, "pr")
         ts_sb = sb.tile([P, N], F32, name="ts_sb", align_bytes=64)
         nc.scalar.copy(ts_sb[:], ts_wide[:])
 
         ks = sb.tile([P, N], U8, name="ks", align_bytes=64)
         nc.vector.tensor_copy(ks[:], ks_pool[:].bitcast(U8).indirect(offsets[:]))
 
-        pr_rows = sb.tile([P, N], F32, name="pr_rows", align_bytes=64)
-        pr_turned = ps.tile([P, BLOCKS, P], F32, name="pr_turned")
-        nc.vector.tensor_copy(pr_rows[:], pr_pool[:].indirect(offsets[:]))
-        for h in range(2):
-            turn(pr_rows, pr_turned, h)
-
         q_codes = sb.tile([P, NQ], U32, name="q_codes", align_bytes=64)
         q_scales = sb.tile([P, NQ], U8, name="q_scales", align_bytes=64)
         nc.vector.quantize_mx(q_codes[:].bitcast(FP8X4), q_scales[:], q_bf[:].rearrange("p w j -> p (w j)"))
-        pr_wide = spread(pr_turned, "pr")
 
         kw = [sb.tile([P, HALF], U32, name=f"kw{h}", align_bytes=64) for h in range(2)]
         for h in range(2):

@@ -41,19 +41,19 @@ def tile_attend_sigprior_srt_kernel(tc, qT, k_words, k_scales, ts, pr, offs, out
         warm_out = sb.tile([P, 1], F32, name="warm_out")
 
         nc.sync.dma_start(offsets[:], offs)
+        nc.sync.dma_start(pr_pool[LAST:P, :], pr[0:1, :])
         nc.sync.dma_start(q_raw[:], qT[0].rearrange("(p j) w -> p j w", j=PACK))
         nc.sync.dma_start(kw_pool[:], k_words[0].rearrange("p n t -> p (n t)").bitcast(I32))
 
         nc.vector.memset(ks_pool[:], 0)
         nc.gpsimd.memset(warm[:], 0.0)
         nc.scalar.dma_start(ts_pool[LAST:P, :], ts[0:1, :])
-        nc.scalar.dma_start(pr_pool[LAST:P, :], pr[0:1, :])
         for quad in range(4):
             if quad == 3:
                 nc.scalar.activation(warm_out[:], warm[:], SIGMOID)
             nc.scalar.dma_start(ks_pool[32 * quad : 32 * quad + 4, :], k_scales[0, 4 * quad : 4 * quad + 4, :].bitcast(I32))
-        nc.vector.memset(ts_pool[0:LAST, :], 0.0)
-        nc.vector.memset(pr_pool[0:LAST, :], 0.0)
+        nc.vector.memset(ts_pool[0:LAST, :].bitcast(I32), 0)
+        nc.vector.memset(pr_pool[0:LAST, :].bitcast(I32), 0)
         nc.vector.memset(ident[:], 0.0)
         make_identity(nc, ident[:], nomemset=True)
 

@@ -24,6 +24,10 @@ HALF = N // 2
 BLOCKS = N // P
 
 
+RUN = T // P
+BANKS = T // N
+
+
 def tile_attend_sigprior_srt_kernel(tc, qT, k_words, k_scales, ts, pr, offs, out):
     nc = tc.nc
     with ExitStack() as ctx:
@@ -34,92 +38,85 @@ def tile_attend_sigprior_srt_kernel(tc, qT, k_words, k_scales, ts, pr, offs, out
         ks_pool = sb.tile([P, T // 4], I32, name="ks_pool", align_bytes=64)
         ts_pool = sb.tile([P, T], F32, name="ts_pool", align_bytes=64)
         pr_pool = sb.tile([P, T], F32, name="pr_pool", align_bytes=64)
-        kw_pool = sb.tile([P, T], I32, name="kw_pool", align_bytes=64)
+        kw_pool = sb.tile([P, T], I32, name="kw_pool", tag="kw_pool", align_bytes=64)
+        pr_runs = sb.tile([P, RUN], F32, name="pr_runs", align_bytes=64)
         q_raw = sb.tile([P, PACK, NQ], F32, name="q_raw", align_bytes=64)
         ident = sb.tile([P, P], F32, name="ident", align_bytes=64)
         warm = sb.tile([P, 1], F32, name="warm")
         warm_out = sb.tile([P, 1], F32, name="warm_out")
 
         nc.sync.dma_start(offsets[:], offs)
-        nc.sync.dma_start(pr_pool[LAST:P, :], pr[0:1, :])
+        nc.sync.dma_start(ts_pool[LAST:P, :], ts[0:1, :])
+        nc.vector.memset(ks_pool[:], 0)
+        for quad in range(4):
+            nc.sync.dma_start(ks_pool[32 * quad : 32 * quad + 4, :], k_scales[0, 4 * quad : 4 * quad + 4, :].bitcast(I32))
         nc.sync.dma_start(q_raw[:], qT[0].rearrange("(p j) w -> p j w", j=PACK))
         nc.sync.dma_start(kw_pool[:], k_words[0].rearrange("p n t -> p (n t)").bitcast(I32))
 
-        nc.vector.memset(ks_pool[:], 0)
+        nc.scalar.dma_start(pr_runs[:], pr[0].rearrange("(p j) -> p j", j=RUN))
         nc.gpsimd.memset(warm[:], 0.0)
-        nc.scalar.dma_start(ts_pool[LAST:P, :], ts[0:1, :])
-        for quad in range(4):
-            if quad == 3:
-                nc.scalar.activation(warm_out[:], warm[:], SIGMOID)
-            nc.scalar.dma_start(ks_pool[32 * quad : 32 * quad + 4, :], k_scales[0, 4 * quad : 4 * quad + 4, :].bitcast(I32))
+        make_identity(nc, ident[:])
+        nc.scalar.activation(warm_out[:], warm[:], SIGMOID)
         nc.vector.memset(ts_pool[0:LAST, :].bitcast(I32), 0)
-        nc.vector.memset(pr_pool[0:LAST, :].bitcast(I32), 0)
-        nc.vector.memset(ident[:], 0.0)
-        make_identity(nc, ident[:], nomemset=True)
 
-        def halves(h):
-            return slice(h * HALF, (h + 1) * HALF), offsets[:, h * (HALF // 16) : (h + 1) * (HALF // 16)]
+        def listed(h):
+            return offsets[:, h * (HALF // 16) : (h + 1) * (HALF // 16)]
 
-        def turn(pool, name):
-            rows = sb.tile([P, N], F32, name=name + "_rows", align_bytes=64)
-            nc.vector.tensor_copy(rows[:], pool[:].indirect(offsets[:]))
-            turned = ps.tile([P, BLOCKS, P], F32, name=name + "_turned")
-            for b in range(BLOCKS):
-                nc.tensor.transpose(turned[:, b, :], rows[:, b * P : (b + 1) * P], ident[:])
-            return turned
-
-        def spread(turned, name):
-            column = sb.tile([P, BLOCKS], F32, name=name + "_column")
-            nc.scalar.copy(column[:], turned[:, :, LAST])
-            wide = ps.tile([P, N], F32, name=name + "_wide")
-            for b in range(BLOCKS):
-                nc.tensor.transpose(wide[:, b * P : (b + 1) * P], column[:, b : b + 1].to_broadcast([P, P]), ident[:])
-            return wide
-
-        q_bf = sb.tile([P, NQ, PACK], BF16, name="q_bf", align_bytes=64)
-        nc.scalar.copy(q_bf[:], q_raw[:].rearrange("p j w -> p w j"))
-
-        ts_turned = turn(ts_pool, "ts")
-        pr_turned = turn(pr_pool, "pr")
-        ts_wide = spread(ts_turned, "ts")
-        pr_wide = spread(pr_turned, "pr")
-        ts_sb = sb.tile([P, N], F32, name="ts_sb", align_bytes=64)
-        nc.scalar.copy(ts_sb[:], ts_wide[:])
-
+        ts_rows = sb.tile([P, N], F32, name="ts_rows", align_bytes=64)
+        nc.vector.tensor_copy(ts_rows[:], ts_pool[:].indirect(offsets[:]))
         ks = sb.tile([P, N], U8, name="ks", align_bytes=64)
         nc.vector.tensor_copy(ks[:], ks_pool[:].bitcast(U8).indirect(offsets[:]))
 
+        pr_by_bank = pr_pool[:].rearrange("m (p c j) -> m c p j", c=BANKS, j=PACK)
+        for c in range(BANKS):
+            wide = ps.tile([P, PACK, P], F32, name=f"pr_wide{c}", tag=f"bank{c}")
+            for j in range(PACK):
+                col = PACK * c + j
+                nc.tensor.transpose(wide[:, j, :], pr_runs[:, col : col + 1].to_broadcast([P, P]), ident[:])
+            nc.scalar.copy(pr_by_bank[:, c], wide[:].rearrange("m j p -> m p j"))
+
+        ts_turned = ps.tile([P, BLOCKS, P], F32, name="ts_turned", tag="bank4")
+        for b in range(BLOCKS):
+            nc.tensor.transpose(ts_turned[:, b, :], ts_rows[:, b * P : (b + 1) * P], ident[:])
+        ts_column = sb.tile([P, BLOCKS], F32, name="ts_column")
+        nc.scalar.copy(ts_column[:], ts_turned[:, :, LAST])
+
+        q_bf = sb.tile([P, NQ, PACK], BF16, name="q_bf", align_bytes=64)
+        nc.vector.tensor_copy(
+            q_bf[:, :, :].rearrange("p (c i) t -> p c t i", i=4),
+            q_raw[:, :, :].rearrange("p t (c i) -> p c t i", i=4),
+        )
         q_codes = sb.tile([P, NQ], U32, name="q_codes", align_bytes=64)
         q_scales = sb.tile([P, NQ], U8, name="q_scales", align_bytes=64)
         nc.vector.quantize_mx(q_codes[:].bitcast(FP8X4), q_scales[:], q_bf[:].rearrange("p w j -> p (w j)"))
 
         kw = [sb.tile([P, HALF], U32, name=f"kw{h}", align_bytes=64) for h in range(2)]
         for h in range(2):
-            nc.vector.tensor_copy(kw[h][:], kw_pool[:].bitcast(U32).indirect(halves(h)[1]))
+            nc.vector.tensor_copy(kw[h][:], kw_pool[:].bitcast(U32).indirect(listed(h)))
 
-        parts = [(h, g) for h in range(2) for g in range(2)]
-        scores, scaled, weight = {}, {}, {}
-        for h, g in parts:
-            cols = halves(h)[0]
-            rows = slice(g * P, (g + 1) * P)
-            scores[h, g] = ps.tile([P, HALF], F32, name=f"scores{h}{g}")
+        pr_rows = sb.tile([P, N], F32, name="pr_rows", tag="kw_pool", align_bytes=64)
+        nc.vector.tensor_copy(pr_rows[:], pr_pool[:].indirect(offsets[:]))
+
+        weight = []
+        for b in range(BLOCKS):
+            scores = ps.tile([P, NQ], F32, name=f"scores{b}", tag=f"bank{b}")
             nc.tensor.matmul_mx(
-                scores[h, g][:],
-                lhsT=q_codes[:, rows].bitcast(FP8X4),
-                lhsT_scale=q_scales[:, rows],
-                rhs=kw[h][:].bitcast(FP8X4),
-                rhs_scale=ks[:, cols],
+                scores[:],
+                lhsT=kw[b // 2][:, (b % 2) * P : (b % 2 + 1) * P].bitcast(FP8X4),
+                lhsT_scale=ks[:, b * P : (b + 1) * P],
+                rhs=q_codes[:].bitcast(FP8X4),
+                rhs_scale=q_scales[:],
                 start=True,
                 stop=True,
             )
-        for h, g in parts:
-            cols = halves(h)[0]
-            scaled[h, g] = sb.tile([P, HALF], F32, name=f"scaled{h}{g}")
-            nc.vector.tensor_tensor(scaled[h, g][:], scores[h, g][:], ts_sb[:, cols], MULT)
-            weight[h, g] = sb.tile([P, HALF], F32, name=f"weight{h}{g}")
-            nc.scalar.activation(weight[h, g][:], scaled[h, g][:], SIGMOID)
-        for h, g in parts:
-            cols = halves(h)[0]
-            result = sb.tile([P, HALF], F32, name=f"result{h}{g}")
-            nc.vector.tensor_tensor(result[:], weight[h, g][:], pr_wide[:, cols], MULT)
-            nc.sync.dma_start(out[0, g * P : (g + 1) * P, cols], result[:])
+            weight.append(sb.tile([P, NQ], F32, name=f"weight{b}", align_bytes=64))
+            nc.scalar.activation(weight[b][:], scores[:], SIGMOID, scale=ts_column[:, b : b + 1])
+        for i, (h, g) in enumerate((h, g) for h in range(2) for g in range(2)):
+            cols = slice(h * HALF, (h + 1) * HALF)
+            rows = slice(g * P, (g + 1) * P)
+            turned = ps.tile([P, 2, P], F32, name=f"turned{g}{h}", tag=f"bank{4 + i}")
+            for e in range(2):
+                nc.tensor.transpose(turned[:, e, :], weight[2 * h + e][:, rows], ident[:])
+            result = sb.tile([P, HALF], F32, name=f"result{g}{h}")
+            nc.vector.tensor_tensor(result[:], turned[:].rearrange("p e s -> p (e s)"), pr_rows[:, cols], MULT)
+            nc.sync.dma_start(out[0, rows, cols], result[:])

@@ -47,15 +47,15 @@ def tile_attend_sigprior_srt_kernel(tc, qT, k_words, k_scales, ts, pr, offs, out
 
         nc.sync.dma_start(offsets[:], offs)
         nc.sync.dma_start(ts_pool[LAST:P, :], ts[0:1, :])
-        nc.vector.memset(ks_pool[:], 0)
-        for quad in range(4):
-            nc.sync.dma_start(ks_pool[32 * quad : 32 * quad + 4, :], k_scales[0, 4 * quad : 4 * quad + 4, :].bitcast(I32))
         nc.sync.dma_start(q_raw[:], qT[0].rearrange("(p j) w -> p j w", j=PACK))
         nc.sync.dma_start(kw_pool[:], k_words[0].rearrange("p n t -> p (n t)").bitcast(I32))
 
         nc.scalar.dma_start(pr_runs[:], pr[0].rearrange("(p j) -> p j", j=RUN))
-        nc.gpsimd.memset(warm[:], 0.0)
         make_identity(nc, ident[:])
+        nc.vector.memset(ks_pool[:], 0)
+        nc.vector.memset(warm[:], 0.0)
+        for quad in range(4):
+            nc.scalar.dma_start(ks_pool[32 * quad : 32 * quad + 4, :], k_scales[0, 4 * quad : 4 * quad + 4, :].bitcast(I32))
         nc.scalar.activation(warm_out[:], warm[:], SIGMOID)
         nc.vector.memset(ts_pool[0:LAST, :].bitcast(I32), 0)
 
@@ -64,8 +64,6 @@ def tile_attend_sigprior_srt_kernel(tc, qT, k_words, k_scales, ts, pr, offs, out
 
         ts_rows = sb.tile([P, N], F32, name="ts_rows", align_bytes=64)
         nc.vector.tensor_copy(ts_rows[:], ts_pool[:].indirect(offsets[:]))
-        ks = sb.tile([P, N], U8, name="ks", align_bytes=64)
-        nc.vector.tensor_copy(ks[:], ks_pool[:].bitcast(U8).indirect(offsets[:]))
 
         pr_by_bank = pr_pool[:].rearrange("m (p c j) -> m c p j", c=BANKS, j=PACK)
         for c in range(BANKS):
@@ -75,13 +73,13 @@ def tile_attend_sigprior_srt_kernel(tc, qT, k_words, k_scales, ts, pr, offs, out
                 nc.tensor.transpose(wide[:, j, :], pr_runs[:, col : col + 1].to_broadcast([P, P]), ident[:])
             nc.scalar.copy(pr_by_bank[:, c], wide[:].rearrange("m j p -> m p j"))
 
-        ts_turned = ps.tile([P, BLOCKS, P], F32, name="ts_turned", tag="bank4")
+        ts_turned = ps.tile([P, BLOCKS, P], F32, name="ts_turned", tag="bank7")
         for b in range(BLOCKS):
             nc.tensor.transpose(ts_turned[:, b, :], ts_rows[:, b * P : (b + 1) * P], ident[:])
         ts_column = sb.tile([P, BLOCKS], F32, name="ts_column")
         nc.scalar.copy(ts_column[:], ts_turned[:, :, LAST])
 
-        q_bf = sb.tile([P, NQ, PACK], BF16, name="q_bf", align_bytes=64)
+        q_bf = sb.tile([P, NQ, PACK], BF16, name="q_bf", tag="q_bf", align_bytes=64)
         nc.vector.tensor_copy(
             q_bf[:, :, :].rearrange("p (c i) t -> p c t i", i=4),
             q_raw[:, :, :].rearrange("p t (c i) -> p c t i", i=4),
@@ -90,6 +88,8 @@ def tile_attend_sigprior_srt_kernel(tc, qT, k_words, k_scales, ts, pr, offs, out
         q_scales = sb.tile([P, NQ], U8, name="q_scales", align_bytes=64)
         nc.vector.quantize_mx(q_codes[:].bitcast(FP8X4), q_scales[:], q_bf[:].rearrange("p w j -> p (w j)"))
 
+        ks = sb.tile([P, N], U8, name="ks", tag="q_bf", align_bytes=64)
+        nc.vector.tensor_copy(ks[:], ks_pool[:].bitcast(U8).indirect(offsets[:]))
         kw = [sb.tile([P, HALF], U32, name=f"kw{h}", align_bytes=64) for h in range(2)]
         for h in range(2):
             nc.vector.tensor_copy(kw[h][:], kw_pool[:].bitcast(U32).indirect(listed(h)))

@@ -26,6 +26,7 @@ BLOCKS = N // P
 
 RUN = T // P
 BANKS = T // N
+KS_FIRST, KS_END = 48, 64
 
 
 def tile_attend_sigprior_srt_kernel(tc, qT, k_words, k_scales, ts, pr, offs, out):
@@ -36,7 +37,7 @@ def tile_attend_sigprior_srt_kernel(tc, qT, k_words, k_scales, ts, pr, offs, out
 
         offsets = sb.tile([P, N // 16], U16, name="offsets")
         ks_pool = sb.tile([P, T // 4], I32, name="ks_pool", align_bytes=64)
-        ts_pool = sb.tile([P, T], F32, name="ts_pool", align_bytes=64)
+        ts_pool = sb.tile([P, T], F32, name="ts_pool", tag="ts_pool", align_bytes=64)
         pr_pool = sb.tile([P, T], F32, name="pr_pool", align_bytes=64)
         kw_pool = sb.tile([P, T], I32, name="kw_pool", tag="kw_pool", align_bytes=64)
         pr_runs = sb.tile([P, RUN], F32, name="pr_runs", align_bytes=64)
@@ -46,22 +47,29 @@ def tile_attend_sigprior_srt_kernel(tc, qT, k_words, k_scales, ts, pr, offs, out
         warm_out = sb.tile([P, 1], F32, name="warm_out")
 
         nc.sync.dma_start(offsets[:], offs)
-        nc.sync.dma_start(ts_pool[LAST:P, :], ts[0:1, :])
+        nc.sync.dma_start(ks_pool[KS_FIRST:KS_END, :], k_scales[0].bitcast(I32))
         nc.sync.dma_start(q_raw[:], qT[0].rearrange("(p j) w -> p j w", j=PACK))
         nc.sync.dma_start(kw_pool[:], k_words[0].rearrange("p n t -> p (n t)").bitcast(I32))
 
         nc.scalar.dma_start(pr_runs[:], pr[0].rearrange("(p j) -> p j", j=RUN))
+        nc.scalar.dma_start(ts_pool[LAST:P, :], ts[0:1, :])
+        nc.gpsimd.memset(warm[:], 0.0)
         make_identity(nc, ident[:])
-        nc.vector.memset(ks_pool[:], 0)
-        nc.vector.memset(warm[:], 0.0)
-        for quad in range(4):
-            nc.scalar.dma_start(ks_pool[32 * quad : 32 * quad + 4, :], k_scales[0, 4 * quad : 4 * quad + 4, :].bitcast(I32))
         nc.scalar.activation(warm_out[:], warm[:], SIGMOID)
+        ks = sb.tile([P, N // 4], I32, name="ks", align_bytes=64)
+        nc.vector.memset(ks_pool[0:KS_FIRST, :], 0)
+        nc.vector.memset(ks_pool[KS_END:P, :], 0)
+        nc.vector.memset(ks[:], 0)
         nc.vector.memset(ts_pool[0:LAST, :].bitcast(I32), 0)
 
         def listed(h):
             return offsets[:, h * (HALF // 16) : (h + 1) * (HALF // 16)]
 
+        ks_rows = sb.tile([P, N], U8, name="ks_rows", align_bytes=64)
+        nc.vector.tensor_copy(ks_rows[:], ks_pool[:].bitcast(U8).indirect(offsets[:]))
+        for quad in range(4):
+            first = KS_FIRST + 4 * quad
+            nc.scalar.dma_start(ks[32 * quad : 32 * quad + 4, :], ks_rows[first : first + 4, :].bitcast(I32))
         ts_rows = sb.tile([P, N], F32, name="ts_rows", align_bytes=64)
         nc.vector.tensor_copy(ts_rows[:], ts_pool[:].indirect(offsets[:]))
 
@@ -79,17 +87,12 @@ def tile_attend_sigprior_srt_kernel(tc, qT, k_words, k_scales, ts, pr, offs, out
         ts_column = sb.tile([P, BLOCKS], F32, name="ts_column")
         nc.scalar.copy(ts_column[:], ts_turned[:, :, LAST])
 
-        q_bf = sb.tile([P, NQ, PACK], BF16, name="q_bf", tag="q_bf", align_bytes=64)
-        nc.vector.tensor_copy(
-            q_bf[:, :, :].rearrange("p (c i) t -> p c t i", i=4),
-            q_raw[:, :, :].rearrange("p t (c i) -> p c t i", i=4),
-        )
+        q_bf = sb.tile([P, NQ, PACK], BF16, name="q_bf", tag="ts_pool", align_bytes=64)
+        nc.vector.tensor_copy(q_bf[:], q_raw[:].rearrange("p j w -> p w j"))
         q_codes = sb.tile([P, NQ], U32, name="q_codes", align_bytes=64)
         q_scales = sb.tile([P, NQ], U8, name="q_scales", align_bytes=64)
         nc.vector.quantize_mx(q_codes[:].bitcast(FP8X4), q_scales[:], q_bf[:].rearrange("p w j -> p (w j)"))
 
-        ks = sb.tile([P, N], U8, name="ks", tag="q_bf", align_bytes=64)
-        nc.vector.tensor_copy(ks[:], ks_pool[:].bitcast(U8).indirect(offsets[:]))
         kw = [sb.tile([P, HALF], U32, name=f"kw{h}", align_bytes=64) for h in range(2)]
         for h in range(2):
             nc.vector.tensor_copy(kw[h][:], kw_pool[:].bitcast(U32).indirect(listed(h)))
@@ -103,7 +106,7 @@ def tile_attend_sigprior_srt_kernel(tc, qT, k_words, k_scales, ts, pr, offs, out
             nc.tensor.matmul_mx(
                 scores[:],
                 lhsT=kw[b // 2][:, (b % 2) * P : (b % 2 + 1) * P].bitcast(FP8X4),
-                lhsT_scale=ks[:, b * P : (b + 1) * P],
+                lhsT_scale=ks[:].bitcast(U8)[:, b * P : (b + 1) * P],
                 rhs=q_codes[:].bitcast(FP8X4),
                 rhs_scale=q_scales[:],
                 start=True,

@@ -40,7 +40,7 @@ def tile_attend_sigprior_srt_kernel(tc, qT, k_words, k_scales, ts, pr, offs, out
         ts_pool = sb.tile([P, T], F32, name="ts_pool", tag="ts_pool", align_bytes=64)
         pr_pool = sb.tile([P, T], F32, name="pr_pool", align_bytes=64)
         kw_pool = sb.tile([P, T], I32, name="kw_pool", tag="kw_pool", align_bytes=64)
-        pr_runs = sb.tile([P, RUN], F32, name="pr_runs", align_bytes=64)
+        pr_runs = sb.tile([P, P], F32, name="pr_runs", align_bytes=64)
         q_raw = sb.tile([P, PACK, NQ], F32, name="q_raw", align_bytes=64)
         ident = sb.tile([P, P], F32, name="ident", align_bytes=64)
         warm = sb.tile([P, 1], F32, name="warm")
@@ -51,12 +51,13 @@ def tile_attend_sigprior_srt_kernel(tc, qT, k_words, k_scales, ts, pr, offs, out
         nc.sync.dma_start(q_raw[:], qT[0].rearrange("(p j) w -> p j w", j=PACK))
         nc.sync.dma_start(kw_pool[:], k_words[0].rearrange("p n t -> p (n t)").bitcast(I32))
 
-        nc.scalar.dma_start(pr_runs[:], pr[0].rearrange("(p j) -> p j", j=RUN))
+        nc.scalar.dma_start(pr_runs[P - RUN : P, :], pr[0].rearrange("(j p) -> j p", p=P))
         nc.scalar.dma_start(ts_pool[LAST:P, :], ts[0:1, :])
         nc.gpsimd.memset(warm[:], 0.0)
         make_identity(nc, ident[:])
         nc.scalar.activation(warm_out[:], warm[:], SIGMOID)
         ks = sb.tile([P, N // 4], I32, name="ks", align_bytes=64)
+        nc.vector.memset(pr_runs[0 : P - RUN, :], 0.0)
         nc.vector.memset(ks_pool[0:KS_FIRST, :], 0)
         nc.vector.memset(ks_pool[KS_END:P, :], 0)
         nc.vector.memset(ks[:], 0)
@@ -65,23 +66,27 @@ def tile_attend_sigprior_srt_kernel(tc, qT, k_words, k_scales, ts, pr, offs, out
         def listed(h):
             return offsets[:, h * (HALF // 16) : (h + 1) * (HALF // 16)]
 
+        pr_turned = ps.tile([P, P], F32, name="pr_turned", tag="bank0")
+        nc.tensor.transpose(pr_turned[:], pr_runs[:], ident[:])
+        pr_columns = sb.tile([P, RUN], F32, name="pr_columns", align_bytes=64)
+        nc.scalar.copy(pr_columns[:], pr_turned[:, P - RUN : P])
+
         ks_rows = sb.tile([P, N], U8, name="ks_rows", align_bytes=64)
         nc.vector.tensor_copy(ks_rows[:], ks_pool[:].bitcast(U8).indirect(offsets[:]))
         for quad in range(4):
             first = KS_FIRST + 4 * quad
-            nc.scalar.dma_start(ks[32 * quad : 32 * quad + 4, :], ks_rows[first : first + 4, :].bitcast(I32))
+            nc.sync.dma_start(ks[32 * quad : 32 * quad + 4, :], ks_rows[first : first + 4, :].bitcast(I32))
         ts_rows = sb.tile([P, N], F32, name="ts_rows", align_bytes=64)
         nc.vector.tensor_copy(ts_rows[:], ts_pool[:].indirect(offsets[:]))
 
-        pr_by_bank = pr_pool[:].rearrange("m (p c j) -> m c p j", c=BANKS, j=PACK)
         for c in range(BANKS):
-            wide = ps.tile([P, PACK, P], F32, name=f"pr_wide{c}", tag=f"bank{c}")
+            wide = ps.tile([P, PACK, P], F32, name=f"pr_wide{c}", tag=f"bank{4 + c}")
             for j in range(PACK):
                 col = PACK * c + j
-                nc.tensor.transpose(wide[:, j, :], pr_runs[:, col : col + 1].to_broadcast([P, P]), ident[:])
-            nc.scalar.copy(pr_by_bank[:, c], wide[:].rearrange("m j p -> m p j"))
+                nc.tensor.transpose(wide[:, j, :], pr_columns[:, col : col + 1].to_broadcast([P, P]), ident[:])
+            nc.scalar.copy(pr_pool[:, c * N : (c + 1) * N], wide[:].rearrange("m j p -> m (j p)"))
 
-        ts_turned = ps.tile([P, BLOCKS, P], F32, name="ts_turned", tag="bank7")
+        ts_turned = ps.tile([P, BLOCKS, P], F32, name="ts_turned", tag="bank5")
         for b in range(BLOCKS):
             nc.tensor.transpose(ts_turned[:, b, :], ts_rows[:, b * P : (b + 1) * P], ident[:])
         ts_column = sb.tile([P, BLOCKS], F32, name="ts_column")

@@ -37,9 +37,8 @@ def tile_attend_sigprior_srt_kernel(tc, qT, k_words, k_scales, ts, pr, offs, out
 
         offsets = sb.tile([P, N // 16], U16, name="offsets")
         ks_pool = sb.tile([P, T // 4], I32, name="ks_pool", align_bytes=64)
-        ts_pool = sb.tile([P, T], F32, name="ts_pool", tag="ts_pool", align_bytes=64)
-        pr_pool = sb.tile([P, T], F32, name="pr_pool", align_bytes=64)
-        kw_pool = sb.tile([P, T], I32, name="kw_pool", tag="kw_pool", align_bytes=64)
+        ts_pool = sb.tile([P, T], F32, name="ts_pool", align_bytes=64)
+        kw_pool = sb.tile([P, T], I32, name="kw_pool", align_bytes=64)
         pr_runs = sb.tile([P, P], F32, name="pr_runs", align_bytes=64)
         q_raw = sb.tile([P, PACK, NQ], F32, name="q_raw", align_bytes=64)
         ident = sb.tile([P, P], F32, name="ident", align_bytes=64)
@@ -47,12 +46,12 @@ def tile_attend_sigprior_srt_kernel(tc, qT, k_words, k_scales, ts, pr, offs, out
         warm_out = sb.tile([P, 1], F32, name="warm_out")
 
         nc.sync.dma_start(offsets[:], offs)
-        nc.sync.dma_start(ks_pool[KS_FIRST:KS_END, :], k_scales[0].bitcast(I32))
+        nc.sync.dma_start(ts_pool[LAST:P, :], ts[0:1, :])
         nc.sync.dma_start(q_raw[:], qT[0].rearrange("(p j) w -> p j w", j=PACK))
         nc.sync.dma_start(kw_pool[:], k_words[0].rearrange("p n t -> p (n t)").bitcast(I32))
 
         nc.scalar.dma_start(pr_runs[P - RUN : P, :], pr[0].rearrange("(j p) -> j p", p=P))
-        nc.scalar.dma_start(ts_pool[LAST:P, :], ts[0:1, :])
+        nc.scalar.dma_start(ks_pool[KS_FIRST:KS_END, :], k_scales[0].bitcast(I32))
         nc.gpsimd.memset(warm[:], 0.0)
         make_identity(nc, ident[:])
         nc.scalar.activation(warm_out[:], warm[:], SIGMOID)
@@ -66,43 +65,48 @@ def tile_attend_sigprior_srt_kernel(tc, qT, k_words, k_scales, ts, pr, offs, out
         def listed(h):
             return offsets[:, h * (HALF // 16) : (h + 1) * (HALF // 16)]
 
-        pr_turned = ps.tile([P, P], F32, name="pr_turned", tag="bank0")
+        pr_turned = ps.tile([P, P], F32, name="pr_turned", tag="bank7")
         nc.tensor.transpose(pr_turned[:], pr_runs[:], ident[:])
         pr_columns = sb.tile([P, RUN], F32, name="pr_columns", align_bytes=64)
         nc.scalar.copy(pr_columns[:], pr_turned[:, P - RUN : P])
 
-        ks_rows = sb.tile([P, N], U8, name="ks_rows", align_bytes=64)
+        ks_rows = sb.tile([P, N], U8, name="ks_rows", tag="ks_rows", align_bytes=64)
         nc.vector.tensor_copy(ks_rows[:], ks_pool[:].bitcast(U8).indirect(offsets[:]))
         for quad in range(4):
             first = KS_FIRST + 4 * quad
             nc.sync.dma_start(ks[32 * quad : 32 * quad + 4, :], ks_rows[first : first + 4, :].bitcast(I32))
+        pr_pool = sb.tile([P, T], F32, name="pr_pool", align_bytes=64)
         ts_rows = sb.tile([P, N], F32, name="ts_rows", align_bytes=64)
         nc.vector.tensor_copy(ts_rows[:], ts_pool[:].indirect(offsets[:]))
 
         for c in range(BANKS):
-            wide = ps.tile([P, PACK, P], F32, name=f"pr_wide{c}", tag=f"bank{4 + c}")
+            wide = ps.tile([P, PACK, P], F32, name=f"pr_wide{c}", tag=("bank4", "bank5", "bank6", "bank2")[c])
             for j in range(PACK):
                 col = PACK * c + j
                 nc.tensor.transpose(wide[:, j, :], pr_columns[:, col : col + 1].to_broadcast([P, P]), ident[:])
             nc.scalar.copy(pr_pool[:, c * N : (c + 1) * N], wide[:].rearrange("m j p -> m (j p)"))
 
-        ts_turned = ps.tile([P, BLOCKS, P], F32, name="ts_turned", tag="bank5")
+        ts_turned = ps.tile([P, BLOCKS, P], F32, name="ts_turned", tag="bank7")
         for b in range(BLOCKS):
             nc.tensor.transpose(ts_turned[:, b, :], ts_rows[:, b * P : (b + 1) * P], ident[:])
         ts_column = sb.tile([P, BLOCKS], F32, name="ts_column")
         nc.scalar.copy(ts_column[:], ts_turned[:, :, LAST])
 
-        q_bf = sb.tile([P, NQ, PACK], BF16, name="q_bf", tag="ts_pool", align_bytes=64)
-        nc.vector.tensor_copy(q_bf[:], q_raw[:].rearrange("p j w -> p w j"))
+        q_bf = sb.tile([P, NQ, PACK], BF16, name="q_bf", align_bytes=64)
+        for g in range(2):
+            rows = slice(g * P, (g + 1) * P)
+            nc.vector.tensor_copy(q_bf[:, rows, :], q_raw[:, :, rows].rearrange("p j w -> p w j"))
         q_codes = sb.tile([P, NQ], U32, name="q_codes", align_bytes=64)
         q_scales = sb.tile([P, NQ], U8, name="q_scales", align_bytes=64)
-        nc.vector.quantize_mx(q_codes[:].bitcast(FP8X4), q_scales[:], q_bf[:].rearrange("p w j -> p (w j)"))
+        for g in range(2):
+            rows = slice(g * P, (g + 1) * P)
+            nc.vector.quantize_mx(q_codes[:, rows].bitcast(FP8X4), q_scales[:, rows], q_bf[:, rows, :].rearrange("p w j -> p (w j)"))
 
         kw = [sb.tile([P, HALF], U32, name=f"kw{h}", align_bytes=64) for h in range(2)]
         for h in range(2):
             nc.vector.tensor_copy(kw[h][:], kw_pool[:].bitcast(U32).indirect(listed(h)))
 
-        pr_rows = sb.tile([P, N], F32, name="pr_rows", tag="kw_pool", align_bytes=64)
+        pr_rows = sb.tile([P, N], F32, name="pr_rows", tag="ks_rows", align_bytes=64)
         nc.vector.tensor_copy(pr_rows[:], pr_pool[:].indirect(offsets[:]))
 
         weight = []
@@ -122,7 +126,7 @@ def tile_attend_sigprior_srt_kernel(tc, qT, k_words, k_scales, ts, pr, offs, out
         for i, (h, g) in enumerate((h, g) for h in range(2) for g in range(2)):
             cols = slice(h * HALF, (h + 1) * HALF)
             rows = slice(g * P, (g + 1) * P)
-            turned = ps.tile([P, 2, P], F32, name=f"turned{g}{h}", tag=f"bank{4 + i}")
+            turned = ps.tile([P, 2, P], F32, name=f"turned{g}{h}", tag=f"bank{2 * h + 1 if g else 4 + h}")
             for e in range(2):
                 nc.tensor.transpose(turned[:, e, :], weight[2 * h + e][:, rows], ident[:])
             result = sb.tile([P, HALF], F32, name=f"result{g}{h}")

@@ -16,119 +16,113 @@ U8 = mybir.dt.uint8
 FP8X4 = mybir.dt.float8_e4m3fn_x4
 MULT = mybir.AluOpType.mult
 SIGMOID = mybir.ActivationFunctionType.Sigmoid
+COPY = mybir.ActivationFunctionType.Copy
 
 P = 128
 PACK = 4
 LAST = P - 1
 HALF = N // 2
 BLOCKS = N // P
-
-
-RUN = T // P
-BANKS = T // N
 KS_FIRST, KS_END = 48, 64
+PR_EARLY = 640
 
 
 def tile_attend_sigprior_srt_kernel(tc, qT, k_words, k_scales, ts, pr, offs, out):
     nc = tc.nc
     with ExitStack() as ctx:
         sb = ctx.enter_context(tc.tile_pool(name="sb", bufs=1))
+        reuse = ctx.enter_context(tc.tile_pool(name="reuse", bufs=1))
         ps = ctx.enter_context(tc.psum_pool(name="ps", bufs=1))
 
         offsets = sb.tile([P, N // 16], U16, name="offsets")
-        ks_pool = sb.tile([P, T // 4], I32, name="ks_pool", align_bytes=64)
-        ts_pool = sb.tile([P, T], F32, name="ts_pool", align_bytes=64)
+        ks_pool = reuse.tile([P, T // 4], I32, name="ks_pool", align_bytes=64, offset=0)
+        ts_pool = reuse.tile([P, T], F32, name="ts_pool", align_bytes=64, offset=5 * T)
+        pr_pool = reuse.tile([P, T], F32, name="pr_pool", align_bytes=64, offset=T)
         kw_pool = sb.tile([P, T], I32, name="kw_pool", align_bytes=64)
-        pr_runs = sb.tile([P, P], F32, name="pr_runs", align_bytes=64)
         q_raw = sb.tile([P, PACK, NQ], F32, name="q_raw", align_bytes=64)
         ident = sb.tile([P, P], F32, name="ident", align_bytes=64)
         warm = sb.tile([P, 1], F32, name="warm")
         warm_out = sb.tile([P, 1], F32, name="warm_out")
+        ks = sb.tile([P, N // 4], I32, name="ks", align_bytes=64)
 
         nc.sync.dma_start(offsets[:], offs)
-        nc.sync.dma_start(ts_pool[LAST:P, :], ts[0:1, :])
+        nc.sync.dma_start(pr_pool[LAST:P, :], pr[0:1, :])
         nc.sync.dma_start(q_raw[:], qT[0].rearrange("(p j) w -> p j w", j=PACK))
         nc.sync.dma_start(kw_pool[:], k_words[0].rearrange("p n t -> p (n t)").bitcast(I32))
-
-        nc.scalar.dma_start(pr_runs[P - RUN : P, :], pr[0].rearrange("(j p) -> j p", p=P))
         nc.scalar.dma_start(ks_pool[KS_FIRST:KS_END, :], k_scales[0].bitcast(I32))
+        nc.scalar.dma_start(ts_pool[LAST:P, :], ts[0:1, :])
         nc.gpsimd.memset(warm[:], 0.0)
-        make_identity(nc, ident[:])
         nc.scalar.activation(warm_out[:], warm[:], SIGMOID)
-        ks = sb.tile([P, N // 4], I32, name="ks", align_bytes=64)
-        nc.vector.memset(pr_runs[0 : P - RUN, :], 0.0)
         nc.vector.memset(ks_pool[0:KS_FIRST, :], 0)
         nc.vector.memset(ks_pool[KS_END:P, :], 0)
         nc.vector.memset(ks[:], 0)
+        nc.vector.memset(pr_pool[0:LAST, 0:PR_EARLY].bitcast(I32), 0)
         nc.vector.memset(ts_pool[0:LAST, :].bitcast(I32), 0)
+        nc.vector.memset(ident[:], 0.0)
+        make_identity(nc, ident[:], nomemset=True)
 
-        def listed(h):
-            return offsets[:, h * (HALF // 16) : (h + 1) * (HALF // 16)]
-
-        pr_turned = ps.tile([P, P], F32, name="pr_turned", tag="bank7")
-        nc.tensor.transpose(pr_turned[:], pr_runs[:], ident[:])
-        pr_columns = sb.tile([P, RUN], F32, name="pr_columns", align_bytes=64)
-        nc.scalar.copy(pr_columns[:], pr_turned[:, P - RUN : P])
-
-        ks_rows = sb.tile([P, N], U8, name="ks_rows", tag="ks_rows", align_bytes=64)
+        ks_rows = sb.tile([P, N], U8, name="ks_rows", align_bytes=64)
         nc.vector.tensor_copy(ks_rows[:], ks_pool[:].bitcast(U8).indirect(offsets[:]))
+        nc.vector.memset(pr_pool[0:LAST, PR_EARLY:T].bitcast(I32), 0)
         for quad in range(4):
             first = KS_FIRST + 4 * quad
             nc.sync.dma_start(ks[32 * quad : 32 * quad + 4, :], ks_rows[first : first + 4, :].bitcast(I32))
-        pr_pool = sb.tile([P, T], F32, name="pr_pool", align_bytes=64)
-        ts_rows = sb.tile([P, N], F32, name="ts_rows", align_bytes=64)
-        nc.vector.tensor_copy(ts_rows[:], ts_pool[:].indirect(offsets[:]))
 
-        for c in range(BANKS):
-            wide = ps.tile([P, PACK, P], F32, name=f"pr_wide{c}", tag=("bank4", "bank5", "bank6", "bank2")[c])
-            for j in range(PACK):
-                col = PACK * c + j
-                nc.tensor.transpose(wide[:, j, :], pr_columns[:, col : col + 1].to_broadcast([P, P]), ident[:])
-            nc.scalar.copy(pr_pool[:, c * N : (c + 1) * N], wide[:].rearrange("m j p -> m (j p)"))
+        columns = []
+        for name, pool, bank, place in (("ts", ts_pool, "bank7", 9 * T), ("pr", pr_pool, "bank6", 5 * T)):
+            rows = reuse.tile([P, N], F32, name=f"{name}_rows", align_bytes=64, offset=place)
+            nc.scalar.activation(rows[:], pool[:].indirect(offsets[:]), COPY)
+            turned = ps.tile([P, BLOCKS, P], F32, name=f"{name}_turned", tag=bank)
+            for b in range(BLOCKS):
+                nc.tensor.transpose(turned[:, b, :], rows[:, b * P : (b + 1) * P], ident[:])
+            columns.append((turned, reuse.tile([P, BLOCKS], F32, name=f"{name}_column", align_bytes=64, offset=T + 64 * len(columns))))
+        for turned, column in columns:
+            nc.scalar.copy(column[:], turned[:, :, LAST])
+        ts_column, pr_column = columns[0][1], columns[1][1]
 
-        ts_turned = ps.tile([P, BLOCKS, P], F32, name="ts_turned", tag="bank7")
-        for b in range(BLOCKS):
-            nc.tensor.transpose(ts_turned[:, b, :], ts_rows[:, b * P : (b + 1) * P], ident[:])
-        ts_column = sb.tile([P, BLOCKS], F32, name="ts_column")
-        nc.scalar.copy(ts_column[:], ts_turned[:, :, LAST])
-
-        q_bf = sb.tile([P, NQ, PACK], BF16, name="q_bf", align_bytes=64)
+        q_bf = reuse.tile([P, NQ, PACK], BF16, name="q_bf", align_bytes=64, offset=0)
         for g in range(2):
             rows = slice(g * P, (g + 1) * P)
-            nc.vector.tensor_copy(q_bf[:, rows, :], q_raw[:, :, rows].rearrange("p j w -> p w j"))
+            nc.vector.tensor_copy(
+                q_bf[:, rows, :].rearrange("p (c i) j -> p c j i", i=4),
+                q_raw[:, :, rows].rearrange("p j (c i) -> p c j i", i=4),
+            )
         q_codes = sb.tile([P, NQ], U32, name="q_codes", align_bytes=64)
         q_scales = sb.tile([P, NQ], U8, name="q_scales", align_bytes=64)
         for g in range(2):
             rows = slice(g * P, (g + 1) * P)
             nc.vector.quantize_mx(q_codes[:, rows].bitcast(FP8X4), q_scales[:, rows], q_bf[:, rows, :].rearrange("p w j -> p (w j)"))
 
-        kw = [sb.tile([P, HALF], U32, name=f"kw{h}", align_bytes=64) for h in range(2)]
-        for h in range(2):
-            nc.vector.tensor_copy(kw[h][:], kw_pool[:].bitcast(U32).indirect(listed(h)))
-
-        pr_rows = sb.tile([P, N], F32, name="pr_rows", tag="ks_rows", align_bytes=64)
-        nc.vector.tensor_copy(pr_rows[:], pr_pool[:].indirect(offsets[:]))
+        kw = [reuse.tile([P, P], U32, name=f"kw{b}", align_bytes=64, offset=4 * P * b) for b in range(BLOCKS)]
+        for b in range(BLOCKS):
+            nc.vector.tensor_copy(kw[b][:], kw_pool[:].bitcast(U32).indirect(offsets[:, b * (P // 16) : (b + 1) * (P // 16)]))
 
         weight = []
         for b in range(BLOCKS):
             scores = ps.tile([P, NQ], F32, name=f"scores{b}", tag=f"bank{b}")
             nc.tensor.matmul_mx(
                 scores[:],
-                lhsT=kw[b // 2][:, (b % 2) * P : (b % 2 + 1) * P].bitcast(FP8X4),
+                lhsT=kw[b][:].bitcast(FP8X4),
                 lhsT_scale=ks[:].bitcast(U8)[:, b * P : (b + 1) * P],
                 rhs=q_codes[:].bitcast(FP8X4),
                 rhs_scale=q_scales[:],
                 start=True,
                 stop=True,
             )
+            gate = sb.tile([P, NQ], F32, name=f"gate{b}", align_bytes=64)
+            nc.scalar.activation(gate[:], scores[:], SIGMOID, scale=ts_column[:, b : b + 1])
             weight.append(sb.tile([P, NQ], F32, name=f"weight{b}", align_bytes=64))
-            nc.scalar.activation(weight[b][:], scores[:], SIGMOID, scale=ts_column[:, b : b + 1])
-        for i, (h, g) in enumerate((h, g) for h in range(2) for g in range(2)):
+            nc.vector.tensor_scalar_mul(weight[b][:], gate[:], pr_column[:, b : b + 1])
+        for h in range(2):
             cols = slice(h * HALF, (h + 1) * HALF)
-            rows = slice(g * P, (g + 1) * P)
-            turned = ps.tile([P, 2, P], F32, name=f"turned{g}{h}", tag=f"bank{2 * h + 1 if g else 4 + h}")
+            turned = [ps.tile([P, 2, P], F32, name=f"turned{g}{h}", tag=f"bank{4 + 2 * h + g}") for g in range(2)]
             for e in range(2):
-                nc.tensor.transpose(turned[:, e, :], weight[2 * h + e][:, rows], ident[:])
-            result = sb.tile([P, HALF], F32, name=f"result{g}{h}")
-            nc.vector.tensor_tensor(result[:], turned[:].rearrange("p e s -> p (e s)"), pr_rows[:, cols], MULT)
-            nc.sync.dma_start(out[0, rows, cols], result[:])
+                for g in range(2):
+                    nc.tensor.transpose(turned[g][:, e, :], weight[2 * h + e][:, g * P : (g + 1) * P], ident[:])
+            for g in range(2):
+                result = sb.tile([P, HALF], F32, name=f"result{g}{h}")
+                if g == 0:
+                    nc.scalar.copy(result[:], turned[g][:].rearrange("p e s -> p (e s)"))
+                else:
+                    nc.vector.tensor_copy(result[:], turned[g][:].rearrange("p e s -> p (e s)"))
+                nc.sync.dma_start(out[0, g * P : (g + 1) * P, cols], result[:])

@@ -23,8 +23,8 @@ PACK = 4
 LAST = P - 1
 HALF = N // 2
 BLOCKS = N // P
-KS_FIRST, KS_END = 48, 64
-PR_EARLY = 640
+KS_FIRST = 112
+PR_PIECE = 512
 
 
 def tile_attend_sigprior_srt_kernel(tc, qT, k_words, k_scales, ts, pr, offs, out):
@@ -49,21 +49,21 @@ def tile_attend_sigprior_srt_kernel(tc, qT, k_words, k_scales, ts, pr, offs, out
         nc.sync.dma_start(pr_pool[LAST:P, :], pr[0:1, :])
         nc.sync.dma_start(q_raw[:], qT[0].rearrange("(p j) w -> p j w", j=PACK))
         nc.sync.dma_start(kw_pool[:], k_words[0].rearrange("p n t -> p (n t)").bitcast(I32))
-        nc.scalar.dma_start(ks_pool[KS_FIRST:KS_END, :], k_scales[0].bitcast(I32))
+        nc.scalar.dma_start(ks_pool[KS_FIRST:P, :], k_scales[0].bitcast(I32))
         nc.scalar.dma_start(ts_pool[LAST:P, :], ts[0:1, :])
         nc.gpsimd.memset(warm[:], 0.0)
         nc.scalar.activation(warm_out[:], warm[:], SIGMOID)
-        nc.vector.memset(ks_pool[0:KS_FIRST, :], 0)
-        nc.vector.memset(ks_pool[KS_END:P, :], 0)
-        nc.vector.memset(ks[:], 0)
-        nc.vector.memset(pr_pool[0:LAST, 0:PR_EARLY].bitcast(I32), 0)
-        nc.vector.memset(ts_pool[0:LAST, :].bitcast(I32), 0)
-        nc.vector.memset(ident[:], 0.0)
-        make_identity(nc, ident[:], nomemset=True)
+        nc.gpsimd.memset(ks_pool[0:KS_FIRST, :], 0)
+        make_identity(nc, ident[:])
+        for first in range(0, T, PR_PIECE):
+            nc.gpsimd.memset(pr_pool[0:LAST, first : first + PR_PIECE].bitcast(I32), 0)
+        nc.vector.memset(ts_pool[0:LAST, 0 : T // 2 - 1].bitcast(I32), 0)
+        nc.vector.memset(ts_pool[0:LAST, T // 2 - 1 : T].bitcast(I32), 0)
+        nc.vector.memset(ks[:, 0 : N // 8 - 1], 0)
+        nc.vector.memset(ks[:, N // 8 - 1 : N // 4], 0)
 
         ks_rows = sb.tile([P, N], U8, name="ks_rows", align_bytes=64)
         nc.vector.tensor_copy(ks_rows[:], ks_pool[:].bitcast(U8).indirect(offsets[:]))
-        nc.vector.memset(pr_pool[0:LAST, PR_EARLY:T].bitcast(I32), 0)
         for quad in range(4):
             first = KS_FIRST + 4 * quad
             nc.sync.dma_start(ks[32 * quad : 32 * quad + 4, :], ks_rows[first : first + 4, :].bitcast(I32))
@@ -71,11 +71,13 @@ def tile_attend_sigprior_srt_kernel(tc, qT, k_words, k_scales, ts, pr, offs, out
         columns = []
         for name, pool, bank, place in (("ts", ts_pool, "bank7", 9 * T), ("pr", pr_pool, "bank6", 5 * T)):
             rows = reuse.tile([P, N], F32, name=f"{name}_rows", align_bytes=64, offset=place)
-            nc.scalar.activation(rows[:], pool[:].indirect(offsets[:]), COPY)
+            for h in range(2):
+                listed = offsets[:, h * (HALF // 16) : (h + 1) * (HALF // 16)]
+                nc.scalar.activation(rows[:, h * HALF : (h + 1) * HALF], pool[:].indirect(listed), COPY)
             turned = ps.tile([P, BLOCKS, P], F32, name=f"{name}_turned", tag=bank)
             for b in range(BLOCKS):
                 nc.tensor.transpose(turned[:, b, :], rows[:, b * P : (b + 1) * P], ident[:])
-            columns.append((turned, reuse.tile([P, BLOCKS], F32, name=f"{name}_column", align_bytes=64, offset=T + 64 * len(columns))))
+            columns.append((turned, reuse.tile([P, BLOCKS], F32, name=f"{name}_column", align_bytes=64, offset=2 * T + 64 * len(columns))))
         for turned, column in columns:
             nc.scalar.copy(column[:], turned[:, :, LAST])
         ts_column, pr_column = columns[0][1], columns[1][1]
@@ -93,16 +95,16 @@ def tile_attend_sigprior_srt_kernel(tc, qT, k_words, k_scales, ts, pr, offs, out
             rows = slice(g * P, (g + 1) * P)
             nc.vector.quantize_mx(q_codes[:, rows].bitcast(FP8X4), q_scales[:, rows], q_bf[:, rows, :].rearrange("p w j -> p (w j)"))
 
-        kw = [reuse.tile([P, P], U32, name=f"kw{b}", align_bytes=64, offset=4 * P * b) for b in range(BLOCKS)]
+        kw = reuse.tile([P, N], U32, name="kw", align_bytes=64, offset=T // 2)
         for b in range(BLOCKS):
-            nc.vector.tensor_copy(kw[b][:], kw_pool[:].bitcast(U32).indirect(offsets[:, b * (P // 16) : (b + 1) * (P // 16)]))
+            nc.vector.tensor_copy(kw[:, b * P : (b + 1) * P], kw_pool[:].bitcast(U32).indirect(offsets[:, b * (P // 16) : (b + 1) * (P // 16)]))
 
         weight = []
         for b in range(BLOCKS):
             scores = ps.tile([P, NQ], F32, name=f"scores{b}", tag=f"bank{b}")
             nc.tensor.matmul_mx(
                 scores[:],
-                lhsT=kw[b][:].bitcast(FP8X4),
+                lhsT=kw[:, b * P : (b + 1) * P].bitcast(FP8X4),
                 lhsT_scale=ks[:].bitcast(U8)[:, b * P : (b + 1) * P],
                 rhs=q_codes[:].bitcast(FP8X4),
                 rhs_scale=q_scales[:],
@@ -113,16 +115,15 @@ def tile_attend_sigprior_srt_kernel(tc, qT, k_words, k_scales, ts, pr, offs, out
             nc.scalar.activation(gate[:], scores[:], SIGMOID, scale=ts_column[:, b : b + 1])
             weight.append(sb.tile([P, NQ], F32, name=f"weight{b}", align_bytes=64))
             nc.vector.tensor_scalar_mul(weight[b][:], gate[:], pr_column[:, b : b + 1])
-        for h in range(2):
+        for i, (h, g) in enumerate((h, g) for h in range(2) for g in range(2)):
             cols = slice(h * HALF, (h + 1) * HALF)
-            turned = [ps.tile([P, 2, P], F32, name=f"turned{g}{h}", tag=f"bank{4 + 2 * h + g}") for g in range(2)]
+            rows = slice(g * P, (g + 1) * P)
+            turned = ps.tile([P, 2, P], F32, name=f"turned{g}{h}", tag=f"bank{4 + i}")
             for e in range(2):
-                for g in range(2):
-                    nc.tensor.transpose(turned[g][:, e, :], weight[2 * h + e][:, g * P : (g + 1) * P], ident[:])
-            for g in range(2):
-                result = sb.tile([P, HALF], F32, name=f"result{g}{h}")
-                if g == 0:
-                    nc.scalar.copy(result[:], turned[g][:].rearrange("p e s -> p (e s)"))
-                else:
-                    nc.vector.tensor_copy(result[:], turned[g][:].rearrange("p e s -> p (e s)"))
-                nc.sync.dma_start(out[0, g * P : (g + 1) * P, cols], result[:])
+                nc.tensor.transpose(turned[:, e, :], weight[2 * h + e][:, rows], ident[:])
+            result = sb.tile([P, HALF], F32, name=f"result{g}{h}")
+            if g == 0:
+                nc.scalar.copy(result[:], turned[:].rearrange("p e s -> p (e s)"))
+            else:
+                nc.vector.tensor_copy(result[:], turned[:].rearrange("p e s -> p (e s)"))
+            nc.sync.dma_start(out[0, rows, cols], result[:])

@@ -24,7 +24,8 @@ LAST = P - 1
 HALF = N // 2
 BLOCKS = N // P
 KS_FIRST = 112
-PR_PIECE = 512
+TS_PIECE = 512
+PREFIX = T - N + HALF
 
 
 def tile_attend_sigprior_srt_kernel(tc, qT, k_words, k_scales, ts, pr, offs, out):
@@ -36,9 +37,9 @@ def tile_attend_sigprior_srt_kernel(tc, qT, k_words, k_scales, ts, pr, offs, out
 
         offsets = sb.tile([P, N // 16], U16, name="offsets")
         ks_pool = reuse.tile([P, T // 4], I32, name="ks_pool", align_bytes=64, offset=0)
-        ts_pool = reuse.tile([P, T], F32, name="ts_pool", align_bytes=64, offset=5 * T)
-        pr_pool = reuse.tile([P, T], F32, name="pr_pool", align_bytes=64, offset=T)
-        kw_pool = sb.tile([P, T], I32, name="kw_pool", align_bytes=64)
+        ts_pool = reuse.tile([P, T], F32, name="ts_pool", align_bytes=64, offset=T)
+        pr_pool = sb.tile([P, T], F32, name="pr_pool", align_bytes=64)
+        kw_pool = sb.tile([P, T], I32, name="kw_pool", tag="kw_pool", align_bytes=64)
         q_raw = sb.tile([P, PACK, NQ], F32, name="q_raw", align_bytes=64)
         ident = sb.tile([P, P], F32, name="ident", align_bytes=64)
         warm = sb.tile([P, 1], F32, name="warm")
@@ -46,19 +47,21 @@ def tile_attend_sigprior_srt_kernel(tc, qT, k_words, k_scales, ts, pr, offs, out
         ks = sb.tile([P, N // 4], I32, name="ks", align_bytes=64)
 
         nc.sync.dma_start(offsets[:], offs)
-        nc.sync.dma_start(pr_pool[LAST:P, :], pr[0:1, :])
+        nc.sync.dma_start(ts_pool[LAST:P, :], ts[0:1, :])
         nc.sync.dma_start(q_raw[:], qT[0].rearrange("(p j) w -> p j w", j=PACK))
-        nc.sync.dma_start(kw_pool[:], k_words[0].rearrange("p n t -> p (n t)").bitcast(I32))
+        words = k_words[0].rearrange("p n t -> p (n t)").bitcast(I32)
+        nc.sync.dma_start(kw_pool[:, 0:PREFIX], words[:, 0:PREFIX])
+        nc.sync.dma_start(kw_pool[:, PREFIX:T], words[:, PREFIX:T])
         nc.scalar.dma_start(ks_pool[KS_FIRST:P, :], k_scales[0].bitcast(I32))
-        nc.scalar.dma_start(ts_pool[LAST:P, :], ts[0:1, :])
+        nc.scalar.dma_start(pr_pool[LAST:P, :], pr[0:1, :])
         nc.gpsimd.memset(warm[:], 0.0)
         nc.scalar.activation(warm_out[:], warm[:], SIGMOID)
         nc.gpsimd.memset(ks_pool[0:KS_FIRST, :], 0)
         make_identity(nc, ident[:])
-        for first in range(0, T, PR_PIECE):
-            nc.gpsimd.memset(pr_pool[0:LAST, first : first + PR_PIECE].bitcast(I32), 0)
-        nc.vector.memset(ts_pool[0:LAST, 0 : T // 2 - 1].bitcast(I32), 0)
-        nc.vector.memset(ts_pool[0:LAST, T // 2 - 1 : T].bitcast(I32), 0)
+        for first in range(0, T, TS_PIECE):
+            nc.gpsimd.memset(ts_pool[0:LAST, first : first + TS_PIECE].bitcast(I32), 0)
+        nc.vector.memset(pr_pool[0:LAST, 0 : T // 2 - 1].bitcast(I32), 0)
+        nc.vector.memset(pr_pool[0:LAST, T // 2 - 1 : T].bitcast(I32), 0)
         nc.vector.memset(ks[:, 0 : N // 8 - 1], 0)
         nc.vector.memset(ks[:, N // 8 - 1 : N // 4], 0)
 
@@ -68,19 +71,34 @@ def tile_attend_sigprior_srt_kernel(tc, qT, k_words, k_scales, ts, pr, offs, out
             first = KS_FIRST + 4 * quad
             nc.sync.dma_start(ks[32 * quad : 32 * quad + 4, :], ks_rows[first : first + 4, :].bitcast(I32))
 
-        columns = []
-        for name, pool, bank, place in (("ts", ts_pool, "bank7", 9 * T), ("pr", pr_pool, "bank6", 5 * T)):
-            rows = reuse.tile([P, N], F32, name=f"{name}_rows", align_bytes=64, offset=place)
-            for h in range(2):
-                listed = offsets[:, h * (HALF // 16) : (h + 1) * (HALF // 16)]
-                nc.scalar.activation(rows[:, h * HALF : (h + 1) * HALF], pool[:].indirect(listed), COPY)
-            turned = ps.tile([P, BLOCKS, P], F32, name=f"{name}_turned", tag=bank)
-            for b in range(BLOCKS):
-                nc.tensor.transpose(turned[:, b, :], rows[:, b * P : (b + 1) * P], ident[:])
-            columns.append((turned, reuse.tile([P, BLOCKS], F32, name=f"{name}_column", align_bytes=64, offset=2 * T + 64 * len(columns))))
-        for turned, column in columns:
-            nc.scalar.copy(column[:], turned[:, :, LAST])
-        ts_column, pr_column = columns[0][1], columns[1][1]
+        def listed(first, count):
+            return offsets[:, first // 16 : (first + count) // 16]
+
+        pr_row = sb.tile([P, N], F32, name="pr_row", tag="pr_row", align_bytes=64)
+        for h in range(2):
+            nc.scalar.activation(pr_row[:, h * HALF : (h + 1) * HALF], pr_pool[:].indirect(listed(h * HALF, HALF)), COPY)
+        pr_turned = ps.tile([P, BLOCKS, P], F32, name="pr_turned", tag="bank5")
+        for b in range(BLOCKS):
+            nc.tensor.transpose(pr_turned[:, b, :], pr_row[:, b * P : (b + 1) * P], ident[:])
+        pr_column = sb.tile([P, BLOCKS], F32, name="pr_column", align_bytes=64)
+        nc.vector.tensor_copy(pr_column[:], pr_turned[:, :, LAST])
+
+        ts_row = sb.tile([P, N], F32, name="ts_row", align_bytes=64)
+        for h in range(2):
+            nc.scalar.activation(ts_row[:, h * HALF : (h + 1) * HALF], ts_pool[:].indirect(listed(h * HALF, HALF)), COPY)
+        first = ps.tile([P, BLOCKS, P], F32, name="first", tag="bank6")
+        second = ps.tile([P, BLOCKS, P], F32, name="second", tag="bank7")
+        ts_place = [first[:, 3, :], second[:, 1, :], second[:, 2, :], second[:, 3, :]]
+        pr_place = [first[:, 0, :], first[:, 1, :], first[:, 2, :], second[:, 0, :]]
+        for b in range(2):
+            nc.tensor.transpose(ts_place[b], ts_row[:, b * P : (b + 1) * P], ident[:])
+        for b in range(BLOCKS):
+            nc.tensor.transpose(pr_place[b], pr_column[:, b : b + 1].to_broadcast([P, P]), ident[:])
+        for b in range(2, BLOCKS):
+            nc.tensor.transpose(ts_place[b], ts_row[:, b * P : (b + 1) * P], ident[:])
+        ts_column = sb.tile([P, BLOCKS], F32, name="ts_column", align_bytes=64)
+        nc.scalar.copy(ts_column[:, 0:1], first[:, 3, LAST:P])
+        nc.scalar.copy(ts_column[:, 1:BLOCKS], second[:, 1:BLOCKS, LAST])
 
         q_bf = reuse.tile([P, NQ, PACK], BF16, name="q_bf", align_bytes=64, offset=0)
         for g in range(2):
@@ -89,15 +107,19 @@ def tile_attend_sigprior_srt_kernel(tc, qT, k_words, k_scales, ts, pr, offs, out
                 q_bf[:, rows, :].rearrange("p (c i) j -> p c j i", i=4),
                 q_raw[:, :, rows].rearrange("p j (c i) -> p c j i", i=4),
             )
-        q_codes = sb.tile([P, NQ], U32, name="q_codes", align_bytes=64)
+        q_codes = sb.tile([P, NQ], U32, name="q_codes", tag="pr_row", align_bytes=64)
         q_scales = sb.tile([P, NQ], U8, name="q_scales", align_bytes=64)
         for g in range(2):
             rows = slice(g * P, (g + 1) * P)
             nc.vector.quantize_mx(q_codes[:, rows].bitcast(FP8X4), q_scales[:, rows], q_bf[:, rows, :].rearrange("p w j -> p (w j)"))
 
         kw = reuse.tile([P, N], U32, name="kw", align_bytes=64, offset=T // 2)
-        for b in range(BLOCKS):
-            nc.vector.tensor_copy(kw[:, b * P : (b + 1) * P], kw_pool[:].bitcast(U32).indirect(offsets[:, b * (P // 16) : (b + 1) * (P // 16)]))
+        nc.vector.tensor_copy(kw[:, 0:HALF], kw_pool[:, 0:PREFIX].bitcast(U32).indirect(listed(0, HALF)))
+        for b in range(2, BLOCKS):
+            nc.vector.tensor_copy(kw[:, b * P : (b + 1) * P], kw_pool[:].bitcast(U32).indirect(listed(b * P, P)))
+        pr_rows = sb.tile([P, N], F32, name="pr_rows", tag="kw_pool", align_bytes=64)
+        nc.vector.tensor_copy(pr_rows[:, 0 : 3 * P], first[:, 0:3, :].rearrange("p b s -> p (b s)"))
+        nc.vector.tensor_copy(pr_rows[:, 3 * P : N], second[:, 0, :])
 
         weight = []
         for b in range(BLOCKS):
@@ -111,10 +133,8 @@ def tile_attend_sigprior_srt_kernel(tc, qT, k_words, k_scales, ts, pr, offs, out
                 start=True,
                 stop=True,
             )
-            gate = sb.tile([P, NQ], F32, name=f"gate{b}", align_bytes=64)
-            nc.scalar.activation(gate[:], scores[:], SIGMOID, scale=ts_column[:, b : b + 1])
             weight.append(sb.tile([P, NQ], F32, name=f"weight{b}", align_bytes=64))
-            nc.vector.tensor_scalar_mul(weight[b][:], gate[:], pr_column[:, b : b + 1])
+            nc.scalar.activation(weight[b][:], scores[:], SIGMOID, scale=ts_column[:, b : b + 1])
         for i, (h, g) in enumerate((h, g) for h in range(2) for g in range(2)):
             cols = slice(h * HALF, (h + 1) * HALF)
             rows = slice(g * P, (g + 1) * P)
@@ -122,8 +142,5 @@ def tile_attend_sigprior_srt_kernel(tc, qT, k_words, k_scales, ts, pr, offs, out
             for e in range(2):
                 nc.tensor.transpose(turned[:, e, :], weight[2 * h + e][:, rows], ident[:])
             result = sb.tile([P, HALF], F32, name=f"result{g}{h}")
-            if g == 0:
-                nc.scalar.copy(result[:], turned[:].rearrange("p e s -> p (e s)"))
-            else:
-                nc.vector.tensor_copy(result[:], turned[:].rearrange("p e s -> p (e s)"))
+            nc.vector.tensor_tensor(result[:], turned[:].rearrange("p e s -> p (e s)"), pr_rows[:, cols], MULT)
             nc.sync.dma_start(out[0, rows, cols], result[:])

@@ -24,7 +24,7 @@ LAST = P - 1
 HALF = N // 2
 BLOCKS = N // P
 KS_FIRST = 112
-TS_PIECE = 512
+SWAP = 288
 PREFIX = T - N + HALF
 
 
@@ -47,23 +47,24 @@ def tile_attend_sigprior_srt_kernel(tc, qT, k_words, k_scales, ts, pr, offs, out
         ks = sb.tile([P, N // 4], I32, name="ks", align_bytes=64)
 
         nc.sync.dma_start(offsets[:], offs)
-        nc.sync.dma_start(ts_pool[LAST:P, :], ts[0:1, :])
+        nc.sync.dma_start(pr_pool[LAST:P, :], pr[0:1, :])
         nc.sync.dma_start(q_raw[:], qT[0].rearrange("(p j) w -> p j w", j=PACK))
+        nc.sync.dma_start(ts_pool[LAST:P, :], ts[0:1, :])
         words = k_words[0].rearrange("p n t -> p (n t)").bitcast(I32)
         nc.sync.dma_start(kw_pool[:, 0:PREFIX], words[:, 0:PREFIX])
         nc.sync.dma_start(kw_pool[:, PREFIX:T], words[:, PREFIX:T])
         nc.scalar.dma_start(ks_pool[KS_FIRST:P, :], k_scales[0].bitcast(I32))
-        nc.scalar.dma_start(pr_pool[LAST:P, :], pr[0:1, :])
         nc.gpsimd.memset(warm[:], 0.0)
         nc.scalar.activation(warm_out[:], warm[:], SIGMOID)
+        nc.gpsimd.memset(ident[:], 0.0)
         nc.gpsimd.memset(ks_pool[0:KS_FIRST, :], 0)
-        make_identity(nc, ident[:])
-        for first in range(0, T, TS_PIECE):
-            nc.gpsimd.memset(ts_pool[0:LAST, first : first + TS_PIECE].bitcast(I32), 0)
-        nc.vector.memset(pr_pool[0:LAST, 0 : T // 2 - 1].bitcast(I32), 0)
-        nc.vector.memset(pr_pool[0:LAST, T // 2 - 1 : T].bitcast(I32), 0)
-        nc.vector.memset(ks[:, 0 : N // 8 - 1], 0)
-        nc.vector.memset(ks[:, N // 8 - 1 : N // 4], 0)
+        nc.gpsimd.memset(pr_pool[0:LAST, T - SWAP : T].bitcast(I32), 0)
+        make_identity(nc, ident[:], nomemset=True)
+        nc.gpsimd.memset(ts_pool[0:LAST, :].bitcast(I32), 0)
+        for view, first, end in ((pr_pool[0:LAST, :].bitcast(I32), 0, T - SWAP), (ks[:], 0, N // 4)):
+            middle = (first + end) // 2 + 1
+            nc.vector.memset(view[:, first:middle], 0)
+            nc.vector.memset(view[:, middle:end], 0)
 
         ks_rows = sb.tile([P, N], U8, name="ks_rows", align_bytes=64)
         nc.vector.tensor_copy(ks_rows[:], ks_pool[:].bitcast(U8).indirect(offsets[:]))
@@ -74,59 +75,60 @@ def tile_attend_sigprior_srt_kernel(tc, qT, k_words, k_scales, ts, pr, offs, out
         def listed(first, count):
             return offsets[:, first // 16 : (first + count) // 16]
 
-        pr_row = sb.tile([P, N], F32, name="pr_row", tag="pr_row", align_bytes=64)
+        pr_row = [reuse.tile([P, HALF], F32, name=f"pr_row{h}", align_bytes=64, offset=5 * T + 4 * HALF * h) for h in range(2)]
+        pr_turned = [ps.tile([P, 2, P], F32, name=f"pr_turned{h}", tag=f"bank{4 + h}") for h in range(2)]
         for h in range(2):
-            nc.scalar.activation(pr_row[:, h * HALF : (h + 1) * HALF], pr_pool[:].indirect(listed(h * HALF, HALF)), COPY)
-        pr_turned = ps.tile([P, BLOCKS, P], F32, name="pr_turned", tag="bank5")
-        for b in range(BLOCKS):
-            nc.tensor.transpose(pr_turned[:, b, :], pr_row[:, b * P : (b + 1) * P], ident[:])
-        pr_column = sb.tile([P, BLOCKS], F32, name="pr_column", align_bytes=64)
-        nc.vector.tensor_copy(pr_column[:], pr_turned[:, :, LAST])
+            nc.scalar.activation(pr_row[h][:], pr_pool[:].indirect(listed(h * HALF, HALF)), COPY)
+            for e in range(2):
+                nc.tensor.transpose(pr_turned[h][:, e, :], pr_row[h][:, e * P : (e + 1) * P], ident[:])
+        pr_column = [sb.tile([P, 2], F32, name=f"pr_column{h}", align_bytes=64) for h in range(2)]
+        for h in range(2):
+            nc.vector.tensor_copy(pr_column[h][:], pr_turned[h][:, :, LAST])
 
         ts_row = sb.tile([P, N], F32, name="ts_row", align_bytes=64)
         for h in range(2):
             nc.scalar.activation(ts_row[:, h * HALF : (h + 1) * HALF], ts_pool[:].indirect(listed(h * HALF, HALF)), COPY)
-        first = ps.tile([P, BLOCKS, P], F32, name="first", tag="bank6")
-        second = ps.tile([P, BLOCKS, P], F32, name="second", tag="bank7")
-        ts_place = [first[:, 3, :], second[:, 1, :], second[:, 2, :], second[:, 3, :]]
-        pr_place = [first[:, 0, :], first[:, 1, :], first[:, 2, :], second[:, 0, :]]
-        for b in range(2):
-            nc.tensor.transpose(ts_place[b], ts_row[:, b * P : (b + 1) * P], ident[:])
-        for b in range(BLOCKS):
-            nc.tensor.transpose(pr_place[b], pr_column[:, b : b + 1].to_broadcast([P, P]), ident[:])
+        early = ps.tile([P, 2, P], F32, name="early", tag="bank6")
+        late = ps.tile([P, BLOCKS, P], F32, name="late", tag="bank7")
+        scores = [ps.tile([P, NQ + P], F32, name=f"scores{b}", tag=f"bank{b}") for b in range(BLOCKS)]
+        pr_place = [early[:, 0, :], early[:, 1, :], late[:, 2, :], late[:, 3, :]]
+        ts_place = [late[:, 0, :], late[:, 1, :], scores[0][:, NQ : NQ + P], scores[1][:, NQ : NQ + P]]
+        for h in range(2):
+            for b in (2 * h, 2 * h + 1):
+                nc.tensor.transpose(pr_place[b], pr_column[h][:, b % 2 : b % 2 + 1].to_broadcast([P, P]), ident[:])
+            if h == 0:
+                for b in range(2):
+                    nc.tensor.transpose(ts_place[b], ts_row[:, b * P : (b + 1) * P], ident[:])
         for b in range(2, BLOCKS):
             nc.tensor.transpose(ts_place[b], ts_row[:, b * P : (b + 1) * P], ident[:])
         ts_column = sb.tile([P, BLOCKS], F32, name="ts_column", align_bytes=64)
-        nc.scalar.copy(ts_column[:, 0:1], first[:, 3, LAST:P])
-        nc.scalar.copy(ts_column[:, 1:BLOCKS], second[:, 1:BLOCKS, LAST])
+        nc.scalar.copy(ts_column[:, 0:2], late[:, 0:2, LAST])
 
-        q_bf = reuse.tile([P, NQ, PACK], BF16, name="q_bf", align_bytes=64, offset=0)
+        q_bf = [reuse.tile([P, P, PACK], BF16, name=f"q_bf{g}", align_bytes=64, offset=(6 * T, 5 * T)[g]) for g in range(2)]
         for g in range(2):
-            rows = slice(g * P, (g + 1) * P)
             nc.vector.tensor_copy(
-                q_bf[:, rows, :].rearrange("p (c i) j -> p c j i", i=4),
-                q_raw[:, :, rows].rearrange("p j (c i) -> p c j i", i=4),
+                q_bf[g][:].rearrange("p (c i) j -> p c j i", i=4),
+                q_raw[:, :, g * P : (g + 1) * P].rearrange("p j (c i) -> p c j i", i=4),
             )
-        q_codes = sb.tile([P, NQ], U32, name="q_codes", tag="pr_row", align_bytes=64)
+        q_codes = reuse.tile([P, NQ], U32, name="q_codes", align_bytes=64, offset=5 * T + 4 * HALF)
         q_scales = sb.tile([P, NQ], U8, name="q_scales", align_bytes=64)
         for g in range(2):
             rows = slice(g * P, (g + 1) * P)
-            nc.vector.quantize_mx(q_codes[:, rows].bitcast(FP8X4), q_scales[:, rows], q_bf[:, rows, :].rearrange("p w j -> p (w j)"))
+            nc.vector.quantize_mx(q_codes[:, rows].bitcast(FP8X4), q_scales[:, rows], q_bf[g][:].rearrange("p w j -> p (w j)"))
 
-        kw = reuse.tile([P, N], U32, name="kw", align_bytes=64, offset=T // 2)
-        nc.vector.tensor_copy(kw[:, 0:HALF], kw_pool[:, 0:PREFIX].bitcast(U32).indirect(listed(0, HALF)))
-        for b in range(2, BLOCKS):
-            nc.vector.tensor_copy(kw[:, b * P : (b + 1) * P], kw_pool[:].bitcast(U32).indirect(listed(b * P, P)))
+        kw = [reuse.tile([P, HALF], U32, name=f"kw{h}", align_bytes=64, offset=(6 * T, T)[h]) for h in range(2)]
+        nc.vector.tensor_copy(kw[0][:], kw_pool[:, 0:PREFIX].bitcast(U32).indirect(listed(0, HALF)))
+        for e in range(2):
+            nc.vector.tensor_copy(kw[1][:, e * P : (e + 1) * P], kw_pool[:].bitcast(U32).indirect(listed(HALF + e * P, P)))
         pr_rows = sb.tile([P, N], F32, name="pr_rows", tag="kw_pool", align_bytes=64)
-        nc.vector.tensor_copy(pr_rows[:, 0 : 3 * P], first[:, 0:3, :].rearrange("p b s -> p (b s)"))
-        nc.vector.tensor_copy(pr_rows[:, 3 * P : N], second[:, 0, :])
+        nc.vector.tensor_copy(pr_rows[:, 0:HALF], early[:].rearrange("p b s -> p (b s)"))
+        nc.vector.tensor_copy(pr_rows[:, HALF:N], late[:, 2:BLOCKS, :].rearrange("p b s -> p (b s)"))
 
         weight = []
         for b in range(BLOCKS):
-            scores = ps.tile([P, NQ], F32, name=f"scores{b}", tag=f"bank{b}")
             nc.tensor.matmul_mx(
-                scores[:],
-                lhsT=kw[:, b * P : (b + 1) * P].bitcast(FP8X4),
+                scores[b][:, 0:NQ],
+                lhsT=kw[b // 2][:, (b % 2) * P : (b % 2 + 1) * P].bitcast(FP8X4),
                 lhsT_scale=ks[:].bitcast(U8)[:, b * P : (b + 1) * P],
                 rhs=q_codes[:].bitcast(FP8X4),
                 rhs_scale=q_scales[:],
@@ -134,7 +136,9 @@ def tile_attend_sigprior_srt_kernel(tc, qT, k_words, k_scales, ts, pr, offs, out
                 stop=True,
             )
             weight.append(sb.tile([P, NQ], F32, name=f"weight{b}", align_bytes=64))
-            nc.scalar.activation(weight[b][:], scores[:], SIGMOID, scale=ts_column[:, b : b + 1])
+            nc.scalar.activation(weight[b][:], scores[b][:, 0:NQ], SIGMOID, scale=ts_column[:, b : b + 1])
+            if b < 2:
+                nc.scalar.copy(ts_column[:, 2 + b : 3 + b], ts_place[2 + b][:, LAST:P])
         for i, (h, g) in enumerate((h, g) for h in range(2) for g in range(2)):
             cols = slice(h * HALF, (h + 1) * HALF)
             rows = slice(g * P, (g + 1) * P)

@@ -24,7 +24,6 @@ LAST = P - 1
 HALF = N // 2
 BLOCKS = N // P
 KS_FIRST = 112
-SWAP = 288
 PREFIX = T - N + HALF
 
 
@@ -58,10 +57,9 @@ def tile_attend_sigprior_srt_kernel(tc, qT, k_words, k_scales, ts, pr, offs, out
         nc.scalar.activation(warm_out[:], warm[:], SIGMOID)
         nc.gpsimd.memset(ident[:], 0.0)
         nc.gpsimd.memset(ks_pool[0:KS_FIRST, :], 0)
-        nc.gpsimd.memset(pr_pool[0:LAST, T - SWAP : T].bitcast(I32), 0)
         make_identity(nc, ident[:], nomemset=True)
         nc.gpsimd.memset(ts_pool[0:LAST, :].bitcast(I32), 0)
-        for view, first, end in ((pr_pool[0:LAST, :].bitcast(I32), 0, T - SWAP), (ks[:], 0, N // 4)):
+        for view, first, end in ((pr_pool[0:LAST, :].bitcast(I32), 0, T), (ks[:], 0, N // 4)):
             middle = (first + end) // 2 + 1
             nc.vector.memset(view[:, first:middle], 0)
             nc.vector.memset(view[:, middle:end], 0)

@@ -137,12 +137,13 @@ def tile_attend_sigprior_srt_kernel(tc, qT, k_words, k_scales, ts, pr, offs, out
             nc.scalar.activation(weight[b][:], scores[b][:, 0:NQ], SIGMOID, scale=ts_column[:, b : b + 1])
             if b < 2:
                 nc.scalar.copy(ts_column[:, 2 + b : 3 + b], ts_place[2 + b][:, LAST:P])
-        for i, (h, g) in enumerate((h, g) for h in range(2) for g in range(2)):
-            cols = slice(h * HALF, (h + 1) * HALF)
+        pieces = ((0, 0, 1), (1, 0, 2), (0, 1, 2), (1, 2, 2), (0, 3, 1))
+        for i, (g, first, count) in enumerate(pieces):
             rows = slice(g * P, (g + 1) * P)
-            turned = ps.tile([P, 2, P], F32, name=f"turned{g}{h}", tag=f"bank{4 + i}")
-            for e in range(2):
-                nc.tensor.transpose(turned[:, e, :], weight[2 * h + e][:, rows], ident[:])
-            result = sb.tile([P, HALF], F32, name=f"result{g}{h}")
+            cols = slice(first * P, (first + count) * P)
+            turned = ps.tile([P, count, P], F32, name=f"turned{i}", tag=f"bank{(4 + i) % 8}")
+            for e in range(count):
+                nc.tensor.transpose(turned[:, e, :], weight[first + e][:, rows], ident[:])
+            result = sb.tile([P, count * P], F32, name=f"result{i}")
             nc.vector.tensor_tensor(result[:], turned[:].rearrange("p e s -> p (e s)"), pr_rows[:, cols], MULT)
             nc.sync.dma_start(out[0, rows, cols], result[:])

@@ -22,9 +22,12 @@ P = 128
 PACK = 4
 LAST = P - 1
 HALF = N // 2
-BLOCKS = N // P
-KS_FIRST = 112
 PREFIX = T - N + HALF
+KS_FIRST = 112
+TS_SHARE = 1536
+PR_SHARE = 512
+TS_ROW = 4 * T + 4 * HALF
+PR_ROW = 6 * T + 4 * HALF
 
 
 def tile_attend_sigprior_srt_kernel(tc, qT, k_words, k_scales, ts, pr, offs, out):
@@ -35,34 +38,36 @@ def tile_attend_sigprior_srt_kernel(tc, qT, k_words, k_scales, ts, pr, offs, out
         ps = ctx.enter_context(tc.psum_pool(name="ps", bufs=1))
 
         offsets = sb.tile([P, N // 16], U16, name="offsets")
-        ks_pool = reuse.tile([P, T // 4], I32, name="ks_pool", align_bytes=64, offset=0)
-        ts_pool = reuse.tile([P, T], F32, name="ts_pool", align_bytes=64, offset=T)
-        pr_pool = sb.tile([P, T], F32, name="pr_pool", align_bytes=64)
-        kw_pool = sb.tile([P, T], I32, name="kw_pool", tag="kw_pool", align_bytes=64)
+        ks_pool = sb.tile([P, T // 4], I32, name="ks_pool", align_bytes=64)
+        ts_pool = sb.tile([P, T], F32, name="ts_pool", align_bytes=64)
+        pr_pool = reuse.tile([P, T], F32, name="pr_pool", align_bytes=64, offset=0)
+        kw_pool = sb.tile([P, T], I32, name="kw_pool", align_bytes=64)
         q_raw = sb.tile([P, PACK, NQ], F32, name="q_raw", align_bytes=64)
         ident = sb.tile([P, P], F32, name="ident", align_bytes=64)
         warm = sb.tile([P, 1], F32, name="warm")
         warm_out = sb.tile([P, 1], F32, name="warm_out")
+
         ks = sb.tile([P, N // 4], I32, name="ks", align_bytes=64)
 
-        nc.sync.dma_start(offsets[:], offs)
-        nc.sync.dma_start(pr_pool[LAST:P, :], pr[0:1, :])
-        nc.sync.dma_start(q_raw[:], qT[0].rearrange("(p j) w -> p j w", j=PACK))
-        nc.sync.dma_start(ts_pool[LAST:P, :], ts[0:1, :])
         words = k_words[0].rearrange("p n t -> p (n t)").bitcast(I32)
+        nc.sync.dma_start(offsets[:], offs)
+        nc.sync.dma_start(ts_pool[LAST:P, :], ts[0:1, :])
+        nc.sync.dma_start(q_raw[:], qT[0].rearrange("(p j) w -> p j w", j=PACK))
+        nc.sync.dma_start(pr_pool[LAST:P, :], pr[0:1, :])
         nc.sync.dma_start(kw_pool[:, 0:PREFIX], words[:, 0:PREFIX])
         nc.sync.dma_start(kw_pool[:, PREFIX:T], words[:, PREFIX:T])
         nc.scalar.dma_start(ks_pool[KS_FIRST:P, :], k_scales[0].bitcast(I32))
-        nc.gpsimd.memset(warm[:], 0.0)
+        nc.vector.memset(warm[:], 0.0)
         nc.scalar.activation(warm_out[:], warm[:], SIGMOID)
         nc.gpsimd.memset(ident[:], 0.0)
         nc.gpsimd.memset(ks_pool[0:KS_FIRST, :], 0)
         make_identity(nc, ident[:], nomemset=True)
-        nc.gpsimd.memset(ts_pool[0:LAST, :].bitcast(I32), 0)
-        for view, first, end in ((pr_pool[0:LAST, :].bitcast(I32), 0, T), (ks[:], 0, N // 4)):
-            middle = (first + end) // 2 + 1
-            nc.vector.memset(view[:, first:middle], 0)
-            nc.vector.memset(view[:, middle:end], 0)
+        nc.gpsimd.memset(ts_pool[0:LAST, TS_SHARE:T].bitcast(I32), 0)
+        nc.gpsimd.memset(pr_pool[0:LAST, PR_SHARE:T].bitcast(I32), 0)
+        for view, width in ((ts_pool[0:LAST, :].bitcast(I32), TS_SHARE), (pr_pool[0:LAST, :].bitcast(I32), PR_SHARE), (ks[:], N // 4)):
+            middle = width // 2 + 1
+            nc.vector.memset(view[:, 0:middle], 0)
+            nc.vector.memset(view[:, middle:width], 0)
 
         ks_rows = sb.tile([P, N], U8, name="ks_rows", align_bytes=64)
         nc.vector.tensor_copy(ks_rows[:], ks_pool[:].bitcast(U8).indirect(offsets[:]))
@@ -73,77 +78,89 @@ def tile_attend_sigprior_srt_kernel(tc, qT, k_words, k_scales, ts, pr, offs, out
         def listed(first, count):
             return offsets[:, first // 16 : (first + count) // 16]
 
-        pr_row = [reuse.tile([P, HALF], F32, name=f"pr_row{h}", align_bytes=64, offset=5 * T + 4 * HALF * h) for h in range(2)]
-        pr_turned = [ps.tile([P, 2, P], F32, name=f"pr_turned{h}", tag=f"bank{4 + h}") for h in range(2)]
-        for h in range(2):
-            nc.scalar.activation(pr_row[h][:], pr_pool[:].indirect(listed(h * HALF, HALF)), COPY)
+        def bank(name, number, blocks):
+            return ps.tile([P, blocks, P], F32, name=name, tag=f"bank{number}")
+
+        def turn(name, pool, h, place, turned):
+            row = reuse.tile([P, HALF], F32, name=f"{name}_row{h}", align_bytes=64, offset=place + 4 * HALF * h)
+            nc.scalar.activation(row[:], pool[:].indirect(listed(h * HALF, HALF)), COPY)
             for e in range(2):
-                nc.tensor.transpose(pr_turned[h][:, e, :], pr_row[h][:, e * P : (e + 1) * P], ident[:])
-        pr_column = [sb.tile([P, 2], F32, name=f"pr_column{h}", align_bytes=64) for h in range(2)]
-        for h in range(2):
-            nc.vector.tensor_copy(pr_column[h][:], pr_turned[h][:, :, LAST])
+                nc.tensor.transpose(turned[:, e, :], row[:, e * P : (e + 1) * P], ident[:])
 
-        ts_row = sb.tile([P, N], F32, name="ts_row", align_bytes=64)
-        for h in range(2):
-            nc.scalar.activation(ts_row[:, h * HALF : (h + 1) * HALF], ts_pool[:].indirect(listed(h * HALF, HALF)), COPY)
-        early = ps.tile([P, 2, P], F32, name="early", tag="bank6")
-        late = ps.tile([P, BLOCKS, P], F32, name="late", tag="bank7")
-        scores = [ps.tile([P, NQ + P], F32, name=f"scores{b}", tag=f"bank{b}") for b in range(BLOCKS)]
-        pr_place = [early[:, 0, :], early[:, 1, :], late[:, 2, :], late[:, 3, :]]
-        ts_place = [late[:, 0, :], late[:, 1, :], scores[0][:, NQ : NQ + P], scores[1][:, NQ : NQ + P]]
-        for h in range(2):
-            for b in (2 * h, 2 * h + 1):
-                nc.tensor.transpose(pr_place[b], pr_column[h][:, b % 2 : b % 2 + 1].to_broadcast([P, P]), ident[:])
-            if h == 0:
-                for b in range(2):
-                    nc.tensor.transpose(ts_place[b], ts_row[:, b * P : (b + 1) * P], ident[:])
-        for b in range(2, BLOCKS):
-            nc.tensor.transpose(ts_place[b], ts_row[:, b * P : (b + 1) * P], ident[:])
-        ts_column = sb.tile([P, BLOCKS], F32, name="ts_column", align_bytes=64)
-        nc.scalar.copy(ts_column[:, 0:2], late[:, 0:2, LAST])
+        def pick(name, h, turned, copy, place):
+            column = reuse.tile([P, 2], F32, name=f"{name}_column{h}", align_bytes=64, offset=place)
+            copy(column[:], turned[:, :, LAST])
+            return column
 
-        q_bf = [reuse.tile([P, P, PACK], BF16, name=f"q_bf{g}", align_bytes=64, offset=(6 * T, 5 * T)[g]) for g in range(2)]
+        def spread(column, rows):
+            for e in range(2):
+                nc.tensor.transpose(rows[:, e, :], column[:, e : e + 1].to_broadcast([P, P]), ident[:])
+            return rows.rearrange("p e s -> p (e s)")
+
+        ts_turned = [bank(f"ts_turned{h}", 4 + h, 2)[:] for h in range(2)]
+        pr_turned = [bank(f"pr_turned{h}", 2 * h, 2)[:] for h in range(2)]
+        for h in range(2):
+            turn("ts", ts_pool, h, TS_ROW, ts_turned[h])
+        ts_column = [pick("ts", 0, ts_turned[0], nc.vector.tensor_copy, 8 * T)]
+        ts_spread = [spread(ts_column[0], bank("ts_spread0", 1, 2)[:])]
+        turn("pr", pr_pool, 0, PR_ROW, pr_turned[0])
+        ts_column.append(pick("ts", 1, ts_turned[1], nc.vector.tensor_copy, 8 * T + 192))
+        ts_spread.append(spread(ts_column[1], bank("ts_spread1", 3, 2)[:]))
+        turn("pr", pr_pool, 1, PR_ROW, pr_turned[1])
+        ts_rows = [reuse.tile([P, HALF], F32, name=f"ts_rows{h}", align_bytes=64, offset=(6 * T + 64, PR_ROW + 8 * HALF - 64)[h]) for h in range(2)]
+        pr_column = []
+        for h in range(2):
+            pr_column.append(pick("pr", h, pr_turned[h], nc.scalar.copy, 8 * T + 64 * (1 + h)))
+            nc.scalar.copy(ts_rows[h][:], ts_spread[h])
+        pr_rows = [spread(pr_column[0], bank("pr_spread0", 6, 2)[:])]
+
+        q_bf = [reuse.tile([P, P, PACK], BF16, name=f"q_bf{g}", align_bytes=64, offset=TS_ROW + (-2 * HALF, 6 * HALF)[g]) for g in range(2)]
         for g in range(2):
             nc.vector.tensor_copy(
                 q_bf[g][:].rearrange("p (c i) j -> p c j i", i=4),
                 q_raw[:, :, g * P : (g + 1) * P].rearrange("p j (c i) -> p c j i", i=4),
             )
-        q_codes = reuse.tile([P, NQ], U32, name="q_codes", align_bytes=64, offset=5 * T + 4 * HALF)
+        q_codes = reuse.tile([P, NQ], U32, name="q_codes", align_bytes=64, offset=TS_ROW + 2 * HALF)
         q_scales = sb.tile([P, NQ], U8, name="q_scales", align_bytes=64)
         for g in range(2):
             rows = slice(g * P, (g + 1) * P)
             nc.vector.quantize_mx(q_codes[:, rows].bitcast(FP8X4), q_scales[:, rows], q_bf[g][:].rearrange("p w j -> p (w j)"))
 
-        kw = [reuse.tile([P, HALF], U32, name=f"kw{h}", align_bytes=64, offset=(6 * T, T)[h]) for h in range(2)]
+        kw = [reuse.tile([P, HALF], U32, name=f"kw{h}", align_bytes=64, offset=(TS_ROW - 2 * HALF, 9 * T)[h]) for h in range(2)]
         nc.vector.tensor_copy(kw[0][:], kw_pool[:, 0:PREFIX].bitcast(U32).indirect(listed(0, HALF)))
-        for e in range(2):
-            nc.vector.tensor_copy(kw[1][:, e * P : (e + 1) * P], kw_pool[:].bitcast(U32).indirect(listed(HALF + e * P, P)))
-        pr_rows = sb.tile([P, N], F32, name="pr_rows", tag="kw_pool", align_bytes=64)
-        nc.vector.tensor_copy(pr_rows[:, 0:HALF], early[:].rearrange("p b s -> p (b s)"))
-        nc.vector.tensor_copy(pr_rows[:, HALF:N], late[:, 2:BLOCKS, :].rearrange("p b s -> p (b s)"))
+        nc.vector.tensor_copy(kw[1][:], kw_pool[:].bitcast(U32).indirect(listed(HALF, HALF)))
 
+        pieces = [(g, h) for h in range(2) for g in range(2)]
         weight = []
-        for b in range(BLOCKS):
+
+        def weigh(i):
+            g, h = pieces[i]
+            rows = slice(g * P, (g + 1) * P)
+            scores = ps.tile([P, HALF], F32, name=f"scores{i}", tag=f"bank{i}")
             nc.tensor.matmul_mx(
-                scores[b][:, 0:NQ],
-                lhsT=kw[b // 2][:, (b % 2) * P : (b % 2 + 1) * P].bitcast(FP8X4),
-                lhsT_scale=ks[:].bitcast(U8)[:, b * P : (b + 1) * P],
-                rhs=q_codes[:].bitcast(FP8X4),
-                rhs_scale=q_scales[:],
+                scores[:],
+                lhsT=q_codes[:, rows].bitcast(FP8X4),
+                lhsT_scale=q_scales[:, rows],
+                rhs=kw[h][:].bitcast(FP8X4),
+                rhs_scale=ks[:].bitcast(U8)[:, h * HALF : (h + 1) * HALF],
                 start=True,
                 stop=True,
             )
-            weight.append(sb.tile([P, NQ], F32, name=f"weight{b}", align_bytes=64))
-            nc.scalar.activation(weight[b][:], scores[b][:, 0:NQ], SIGMOID, scale=ts_column[:, b : b + 1])
-            if b < 2:
-                nc.scalar.copy(ts_column[:, 2 + b : 3 + b], ts_place[2 + b][:, LAST:P])
-        pieces = ((0, 0, 1), (1, 0, 2), (0, 1, 2), (1, 2, 2), (0, 3, 1))
-        for i, (g, first, count) in enumerate(pieces):
-            rows = slice(g * P, (g + 1) * P)
-            cols = slice(first * P, (first + count) * P)
-            turned = ps.tile([P, count, P], F32, name=f"turned{i}", tag=f"bank{(4 + i) % 8}")
-            for e in range(count):
-                nc.tensor.transpose(turned[:, e, :], weight[first + e][:, rows], ident[:])
-            result = sb.tile([P, count * P], F32, name=f"result{i}")
-            nc.vector.tensor_tensor(result[:], turned[:].rearrange("p e s -> p (e s)"), pr_rows[:, cols], MULT)
-            nc.sync.dma_start(out[0, rows, cols], result[:])
+            scaled = sb.tile([P, HALF], F32, name=f"scaled{i}", align_bytes=64)
+            nc.vector.tensor_tensor(scaled[:], scores[:], ts_rows[h][:], MULT)
+            weight.append(sb.tile([P, HALF], F32, name=f"weight{i}", align_bytes=64))
+            nc.scalar.activation(weight[i][:], scaled[:], SIGMOID)
+
+        def finish(i):
+            g, h = pieces[i]
+            result = sb.tile([P, HALF], F32, name=f"result{i}", align_bytes=64)
+            nc.vector.tensor_tensor(result[:], weight[i][:], pr_rows[h], MULT)
+            nc.sync.dma_start(out[0, g * P : (g + 1) * P, h * HALF : (h + 1) * HALF], result[:])
+
+        for i in range(3):
+            weigh(i)
+        finish(0)
+        weigh(3)
+        pr_rows.append(spread(pr_column[1], bank("pr_spread1", 0, 2)[:]))
+        for i in range(1, 4):
+            finish(i)

@@ -38,7 +38,7 @@ def tile_attend_sigprior_srt_kernel(tc, qT, k_words, k_scales, ts, pr, offs, out
         ps = ctx.enter_context(tc.psum_pool(name="ps", bufs=1))
 
         offsets = sb.tile([P, N // 16], U16, name="offsets")
-        ks_pool = sb.tile([P, T // 4], I32, name="ks_pool", align_bytes=64)
+        ks_pool = reuse.tile([P, T // 4], I32, name="ks_pool", align_bytes=64, offset=10 * T)
         ts_pool = sb.tile([P, T], F32, name="ts_pool", align_bytes=64)
         pr_pool = reuse.tile([P, T], F32, name="pr_pool", align_bytes=64, offset=0)
         kw_pool = sb.tile([P, T], I32, name="kw_pool", align_bytes=64)
@@ -47,7 +47,6 @@ def tile_attend_sigprior_srt_kernel(tc, qT, k_words, k_scales, ts, pr, offs, out
         warm = sb.tile([P, 1], F32, name="warm")
         warm_out = sb.tile([P, 1], F32, name="warm_out")
 
-        ks = sb.tile([P, N // 4], I32, name="ks", align_bytes=64)
 
         words = k_words[0].rearrange("p n t -> p (n t)").bitcast(I32)
         nc.sync.dma_start(offsets[:], offs)
@@ -64,13 +63,14 @@ def tile_attend_sigprior_srt_kernel(tc, qT, k_words, k_scales, ts, pr, offs, out
         make_identity(nc, ident[:], nomemset=True)
         nc.gpsimd.memset(ts_pool[0:LAST, TS_SHARE:T].bitcast(I32), 0)
         nc.gpsimd.memset(pr_pool[0:LAST, PR_SHARE:T].bitcast(I32), 0)
-        for view, width in ((ts_pool[0:LAST, :].bitcast(I32), TS_SHARE), (pr_pool[0:LAST, :].bitcast(I32), PR_SHARE), (ks[:], N // 4)):
+        for view, width in ((ts_pool[0:LAST, :].bitcast(I32), TS_SHARE), (pr_pool[0:LAST, :].bitcast(I32), PR_SHARE)):
             middle = width // 2 + 1
             nc.vector.memset(view[:, 0:middle], 0)
             nc.vector.memset(view[:, middle:width], 0)
 
         ks_rows = sb.tile([P, N], U8, name="ks_rows", align_bytes=64)
         nc.vector.tensor_copy(ks_rows[:], ks_pool[:].bitcast(U8).indirect(offsets[:]))
+        ks = reuse.tile([P, N // 4], I32, name="ks", align_bytes=64, offset=10 * T)
         for quad in range(4):
             first = KS_FIRST + 4 * quad
             nc.sync.dma_start(ks[32 * quad : 32 * quad + 4, :], ks_rows[first : first + 4, :].bitcast(I32))
@@ -114,19 +114,19 @@ def tile_attend_sigprior_srt_kernel(tc, qT, k_words, k_scales, ts, pr, offs, out
             nc.scalar.copy(ts_rows[h][:], ts_spread[h])
         pr_rows = [spread(pr_column[0], bank("pr_spread0", 6, 2)[:])]
 
-        q_bf = [reuse.tile([P, P, PACK], BF16, name=f"q_bf{g}", align_bytes=64, offset=TS_ROW + (-2 * HALF, 6 * HALF)[g]) for g in range(2)]
+        q_bf = [reuse.tile([P, P, PACK], BF16, name=f"q_bf{g}", align_bytes=64, offset=TS_ROW - 4 * HALF * (1 - g)) for g in range(2)]
         for g in range(2):
             nc.vector.tensor_copy(
                 q_bf[g][:].rearrange("p (c i) j -> p c j i", i=4),
                 q_raw[:, :, g * P : (g + 1) * P].rearrange("p j (c i) -> p c j i", i=4),
             )
-        q_codes = reuse.tile([P, NQ], U32, name="q_codes", align_bytes=64, offset=TS_ROW + 2 * HALF)
+        q_codes = reuse.tile([P, NQ], U32, name="q_codes", align_bytes=64, offset=TS_ROW + 4 * HALF)
         q_scales = sb.tile([P, NQ], U8, name="q_scales", align_bytes=64)
         for g in range(2):
             rows = slice(g * P, (g + 1) * P)
             nc.vector.quantize_mx(q_codes[:, rows].bitcast(FP8X4), q_scales[:, rows], q_bf[g][:].rearrange("p w j -> p (w j)"))
 
-        kw = [reuse.tile([P, HALF], U32, name=f"kw{h}", align_bytes=64, offset=(TS_ROW - 2 * HALF, 9 * T)[h]) for h in range(2)]
+        kw = [reuse.tile([P, HALF], U32, name=f"kw{h}", align_bytes=64, offset=TS_ROW - 4 * HALF * (1 - h)) for h in range(2)]
         nc.vector.tensor_copy(kw[0][:], kw_pool[:, 0:PREFIX].bitcast(U32).indirect(listed(0, HALF)))
         nc.vector.tensor_copy(kw[1][:], kw_pool[:].bitcast(U32).indirect(listed(HALF, HALF)))
 

@@ -113,6 +113,8 @@ def tile_attend_sigprior_srt_kernel(tc, qT, k_words, k_scales, ts, pr, offs, out
             pr_column.append(pick("pr", h, pr_turned[h], nc.scalar.copy, 8 * T + 64 * (1 + h)))
             nc.scalar.copy(ts_rows[h][:], ts_spread[h])
         pr_rows = [spread(pr_column[0], bank("pr_spread0", 6, 2)[:])]
+        pr_first = sb.tile([P, P], F32, name="pr_first", align_bytes=64)
+        nc.scalar.copy(pr_first[:], pr_rows[0][:, 0:P])
 
         q_bf = [reuse.tile([P, P, PACK], BF16, name=f"q_bf{g}", align_bytes=64, offset=TS_ROW - 4 * HALF * (1 - g)) for g in range(2)]
         for g in range(2):
@@ -130,37 +132,41 @@ def tile_attend_sigprior_srt_kernel(tc, qT, k_words, k_scales, ts, pr, offs, out
         nc.vector.tensor_copy(kw[0][:], kw_pool[:, 0:PREFIX].bitcast(U32).indirect(listed(0, HALF)))
         nc.vector.tensor_copy(kw[1][:], kw_pool[:].bitcast(U32).indirect(listed(HALF, HALF)))
 
-        pieces = [(g, h) for h in range(2) for g in range(2)]
+        pieces = ((0, 0, P, 0), (0, P, P, 1), (1, 0, HALF, 2), (0, HALF, HALF, 3), (1, HALF, HALF, 4))
         weight = []
 
         def weigh(i):
-            g, h = pieces[i]
+            g, first, count, number = pieces[i]
+            h, cols = first // HALF, slice(first % HALF, first % HALF + count)
             rows = slice(g * P, (g + 1) * P)
-            scores = ps.tile([P, HALF], F32, name=f"scores{i}", tag=f"bank{i}")
+            scores = ps.tile([P, count], F32, name=f"scores{i}", tag=f"bank{number}")
             nc.tensor.matmul_mx(
                 scores[:],
                 lhsT=q_codes[:, rows].bitcast(FP8X4),
                 lhsT_scale=q_scales[:, rows],
-                rhs=kw[h][:].bitcast(FP8X4),
-                rhs_scale=ks[:].bitcast(U8)[:, h * HALF : (h + 1) * HALF],
+                rhs=kw[h][:, cols].bitcast(FP8X4),
+                rhs_scale=ks[:].bitcast(U8)[:, first : first + count],
                 start=True,
                 stop=True,
             )
-            scaled = sb.tile([P, HALF], F32, name=f"scaled{i}", align_bytes=64)
-            nc.vector.tensor_tensor(scaled[:], scores[:], ts_rows[h][:], MULT)
-            weight.append(sb.tile([P, HALF], F32, name=f"weight{i}", align_bytes=64))
+            scaled = sb.tile([P, count], F32, name=f"scaled{i}", align_bytes=64)
+            nc.vector.tensor_tensor(scaled[:], ts_rows[h][:, cols], scores[:], MULT)
+            weight.append(sb.tile([P, count], F32, name=f"weight{i}", align_bytes=64))
             nc.scalar.activation(weight[i][:], scaled[:], SIGMOID)
 
-        def finish(i):
-            g, h = pieces[i]
-            result = sb.tile([P, HALF], F32, name=f"result{i}", align_bytes=64)
-            nc.vector.tensor_tensor(result[:], weight[i][:], pr_rows[h], MULT)
+        def store(g, h, result):
             nc.sync.dma_start(out[0, g * P : (g + 1) * P, h * HALF : (h + 1) * HALF], result[:])
 
-        for i in range(3):
+        for i in range(4):
             weigh(i)
-        finish(0)
-        weigh(3)
+        result = sb.tile([P, HALF], F32, name="result", align_bytes=64)
+        nc.gpsimd.tensor_tensor(result[:, 0:P], weight[0][:], pr_first[:], MULT)
+        nc.vector.tensor_tensor(result[:, P:HALF], weight[1][:], pr_rows[0][:, P:HALF], MULT)
+        store(0, 0, result)
+        weigh(4)
         pr_rows.append(spread(pr_column[1], bank("pr_spread1", 0, 2)[:]))
-        for i in range(1, 4):
-            finish(i)
+        for i in range(2, 5):
+            g, first, count, number = pieces[i]
+            result = sb.tile([P, HALF], F32, name=f"result{i}", align_bytes=64)
+            nc.vector.tensor_tensor(result[:], weight[i][:], pr_rows[first // HALF], MULT)
+            store(g, first // HALF, result)

from contextlib import ExitStack

import concourse.mybir as mybir
from concourse.masks import make_identity

NQ, N, T, D = 256, 512, 2048, 512
FLOPS = 2 * NQ * N * D
BYTES = 4 * D * NQ + D * T + 16 * T + 2 * 4 * T + 128 * (N // 16) * 2 + 4 * NQ * N

F32 = mybir.dt.float32
BF16 = mybir.dt.bfloat16
I32 = mybir.dt.int32
U32 = mybir.dt.uint32
U16 = mybir.dt.uint16
U8 = mybir.dt.uint8
FP8X4 = mybir.dt.float8_e4m3fn_x4
MULT = mybir.AluOpType.mult
SIGMOID = mybir.ActivationFunctionType.Sigmoid
COPY = mybir.ActivationFunctionType.Copy

P = 128
PACK = 4
LAST = P - 1
HALF = N // 2
PREFIX = T - N + HALF
KS_FIRST = 112
TS_SHARE = 1536
PR_SHARE = 512
TS_ROW = 4 * T + 4 * HALF
PR_ROW = 6 * T + 4 * HALF


def tile_attend_sigprior_srt_kernel(tc, qT, k_words, k_scales, ts, pr, offs, out):
    nc = tc.nc
    with ExitStack() as ctx:
        sb = ctx.enter_context(tc.tile_pool(name="sb", bufs=1))
        reuse = ctx.enter_context(tc.tile_pool(name="reuse", bufs=1))
        ps = ctx.enter_context(tc.psum_pool(name="ps", bufs=1))

        offsets = sb.tile([P, N // 16], U16, name="offsets")
        ks_pool = reuse.tile([P, T // 4], I32, name="ks_pool", align_bytes=64, offset=10 * T)
        ts_pool = sb.tile([P, T], F32, name="ts_pool", align_bytes=64)
        pr_pool = reuse.tile([P, T], F32, name="pr_pool", align_bytes=64, offset=0)
        kw_pool = sb.tile([P, T], I32, name="kw_pool", align_bytes=64)
        q_raw = sb.tile([P, PACK, NQ], F32, name="q_raw", align_bytes=64)
        ident = sb.tile([P, P], F32, name="ident", align_bytes=64)
        warm = sb.tile([P, 1], F32, name="warm")
        warm_out = sb.tile([P, 1], F32, name="warm_out")


        words = k_words[0].rearrange("p n t -> p (n t)").bitcast(I32)
        nc.sync.dma_start(offsets[:], offs)
        nc.sync.dma_start(ts_pool[LAST:P, :], ts[0:1, :])
        nc.sync.dma_start(q_raw[:], qT[0].rearrange("(p j) w -> p j w", j=PACK))
        nc.sync.dma_start(pr_pool[LAST:P, :], pr[0:1, :])
        nc.sync.dma_start(kw_pool[:, 0:PREFIX], words[:, 0:PREFIX])
        nc.sync.dma_start(kw_pool[:, PREFIX:T], words[:, PREFIX:T])
        nc.scalar.dma_start(ks_pool[KS_FIRST:P, :], k_scales[0].bitcast(I32))
        nc.vector.memset(warm[:], 0.0)
        nc.scalar.activation(warm_out[:], warm[:], SIGMOID)
        nc.gpsimd.memset(ident[:], 0.0)
        nc.gpsimd.memset(ks_pool[0:KS_FIRST, :], 0)
        make_identity(nc, ident[:], nomemset=True)
        nc.gpsimd.memset(ts_pool[0:LAST, TS_SHARE:T].bitcast(I32), 0)
        nc.gpsimd.memset(pr_pool[0:LAST, PR_SHARE:T].bitcast(I32), 0)
        for view, width in ((ts_pool[0:LAST, :].bitcast(I32), TS_SHARE), (pr_pool[0:LAST, :].bitcast(I32), PR_SHARE)):
            middle = width // 2 + 1
            nc.vector.memset(view[:, 0:middle], 0)
            nc.vector.memset(view[:, middle:width], 0)

        ks_rows = sb.tile([P, N], U8, name="ks_rows", align_bytes=64)
        nc.vector.tensor_copy(ks_rows[:], ks_pool[:].bitcast(U8).indirect(offsets[:]))
        ks = reuse.tile([P, N // 4], I32, name="ks", align_bytes=64, offset=10 * T)
        for quad in range(4):
            first = KS_FIRST + 4 * quad
            nc.sync.dma_start(ks[32 * quad : 32 * quad + 4, :], ks_rows[first : first + 4, :].bitcast(I32))

        def listed(first, count):
            return offsets[:, first // 16 : (first + count) // 16]

        def bank(name, number, blocks):
            return ps.tile([P, blocks, P], F32, name=name, tag=f"bank{number}")

        def turn(name, pool, h, place, turned):
            row = reuse.tile([P, HALF], F32, name=f"{name}_row{h}", align_bytes=64, offset=place + 4 * HALF * h)
            nc.scalar.activation(row[:], pool[:].indirect(listed(h * HALF, HALF)), COPY)
            for e in range(2):
                nc.tensor.transpose(turned[:, e, :], row[:, e * P : (e + 1) * P], ident[:])

        def pick(name, h, turned, copy, place):
            column = reuse.tile([P, 2], F32, name=f"{name}_column{h}", align_bytes=64, offset=place)
            copy(column[:], turned[:, :, LAST])
            return column

        def spread(column, rows):
            for e in range(2):
                nc.tensor.transpose(rows[:, e, :], column[:, e : e + 1].to_broadcast([P, P]), ident[:])
            return rows.rearrange("p e s -> p (e s)")

        ts_turned = [bank(f"ts_turned{h}", 4 + h, 2)[:] for h in range(2)]
        pr_turned = [bank(f"pr_turned{h}", 2 * h, 2)[:] for h in range(2)]
        for h in range(2):
            turn("ts", ts_pool, h, TS_ROW, ts_turned[h])
        ts_column = [pick("ts", 0, ts_turned[0], nc.vector.tensor_copy, 8 * T)]
        ts_spread = [spread(ts_column[0], bank("ts_spread0", 1, 2)[:])]
        turn("pr", pr_pool, 0, PR_ROW, pr_turned[0])
        ts_column.append(pick("ts", 1, ts_turned[1], nc.vector.tensor_copy, 8 * T + 192))
        ts_spread.append(spread(ts_column[1], bank("ts_spread1", 3, 2)[:]))
        turn("pr", pr_pool, 1, PR_ROW, pr_turned[1])
        ts_rows = [reuse.tile([P, HALF], F32, name=f"ts_rows{h}", align_bytes=64, offset=(6 * T + 64, PR_ROW + 8 * HALF - 64)[h]) for h in range(2)]
        pr_column = []
        for h in range(2):
            pr_column.append(pick("pr", h, pr_turned[h], nc.scalar.copy, 8 * T + 64 * (1 + h)))
            nc.scalar.copy(ts_rows[h][:], ts_spread[h])
        pr_rows = [spread(pr_column[0], bank("pr_spread0", 6, 2)[:])]
        pr_first = sb.tile([P, P], F32, name="pr_first", align_bytes=64)
        nc.scalar.copy(pr_first[:], pr_rows[0][:, 0:P])

        q_bf = [reuse.tile([P, P, PACK], BF16, name=f"q_bf{g}", align_bytes=64, offset=TS_ROW - 4 * HALF * (1 - g)) for g in range(2)]
        for g in range(2):
            nc.vector.tensor_copy(
                q_bf[g][:].rearrange("p (c i) j -> p c j i", i=4),
                q_raw[:, :, g * P : (g + 1) * P].rearrange("p j (c i) -> p c j i", i=4),
            )
        q_codes = reuse.tile([P, NQ], U32, name="q_codes", align_bytes=64, offset=TS_ROW + 4 * HALF)
        q_scales = sb.tile([P, NQ], U8, name="q_scales", align_bytes=64)
        for g in range(2):
            rows = slice(g * P, (g + 1) * P)
            nc.vector.quantize_mx(q_codes[:, rows].bitcast(FP8X4), q_scales[:, rows], q_bf[g][:].rearrange("p w j -> p (w j)"))

        kw = [reuse.tile([P, HALF], U32, name=f"kw{h}", align_bytes=64, offset=TS_ROW - 4 * HALF * (1 - h)) for h in range(2)]
        nc.vector.tensor_copy(kw[0][:], kw_pool[:, 0:PREFIX].bitcast(U32).indirect(listed(0, HALF)))
        nc.vector.tensor_copy(kw[1][:], kw_pool[:].bitcast(U32).indirect(listed(HALF, HALF)))

        pieces = ((0, 0, P, 0), (0, P, P, 1), (1, 0, HALF, 2), (0, HALF, HALF, 3), (1, HALF, HALF, 4))
        weight = []

        def weigh(i):
            g, first, count, number = pieces[i]
            h, cols = first // HALF, slice(first % HALF, first % HALF + count)
            rows = slice(g * P, (g + 1) * P)
            scores = ps.tile([P, count], F32, name=f"scores{i}", tag=f"bank{number}")
            nc.tensor.matmul_mx(
                scores[:],
                lhsT=q_codes[:, rows].bitcast(FP8X4),
                lhsT_scale=q_scales[:, rows],
                rhs=kw[h][:, cols].bitcast(FP8X4),
                rhs_scale=ks[:].bitcast(U8)[:, first : first + count],
                start=True,
                stop=True,
            )
            scaled = sb.tile([P, count], F32, name=f"scaled{i}", align_bytes=64)
            nc.vector.tensor_tensor(scaled[:], ts_rows[h][:, cols], scores[:], MULT)
            weight.append(sb.tile([P, count], F32, name=f"weight{i}", align_bytes=64))
            nc.scalar.activation(weight[i][:], scaled[:], SIGMOID)

        def store(g, h, result):
            nc.sync.dma_start(out[0, g * P : (g + 1) * P, h * HALF : (h + 1) * HALF], result[:])

        for i in range(4):
            weigh(i)
        result = sb.tile([P, HALF], F32, name="result", align_bytes=64)
        nc.gpsimd.tensor_tensor(result[:, 0:P], weight[0][:], pr_first[:], MULT)
        nc.vector.tensor_tensor(result[:, P:HALF], weight[1][:], pr_rows[0][:, P:HALF], MULT)
        store(0, 0, result)
        weigh(4)
        pr_rows.append(spread(pr_column[1], bank("pr_spread1", 0, 2)[:]))
        for i in range(2, 5):
            g, first, count, number = pieces[i]
            result = sb.tile([P, HALF], F32, name=f"result{i}", align_bytes=64)
            nc.vector.tensor_tensor(result[:], weight[i][:], pr_rows[first // HALF], MULT)
            store(g, first // HALF, result)
